import numpy as np
import ml_dtypes


def mxq(x, axis, fmt="e4m3"):
    dtype, down = {"e4m3": (ml_dtypes.float8_e4m3fn, 7), "e5m2": (ml_dtypes.float8_e5m2, 14)}[fmt]
    v = np.moveaxis(np.asarray(x, np.float32).astype(ml_dtypes.bfloat16).astype(np.float64), axis, -1)
    blocks = v.reshape(v.shape[:-1] + (-1, 32))
    amax = np.abs(blocks).max(-1, keepdims=True)
    byte = np.maximum(np.where(amax > 0, np.frexp(amax)[1] - 1 + 127, 0) - down, 1)
    scale = np.exp2(byte - 127.0)
    codes = (blocks / scale).astype(np.float32).astype(dtype).astype(np.float64)
    return np.moveaxis((codes * scale).reshape(v.shape), -1, axis)


WIDE = False


def mx_kscale(k):
    if not WIDE:
        return np.ones(k)
    levels = np.array([10, -10, 5, -5, 0])
    if k % 512:
        return np.exp2(np.random.permutation(np.resize(levels, k // 32))).repeat(32)
    a = np.empty((k // 512, 16))
    for p in range(k // 512):
        a[p, :8] = np.random.permutation(np.resize(levels, 8))
        for g in range(8):
            far = levels[np.abs(levels - a[p, g]) >= 10]
            a[p, g + 8] = far[np.random.randint(len(far))]
    return np.exp2(a.ravel()).repeat(32)


def f64(x):
    return np.asarray(x).astype(np.float64)


def striped(idx):
    return np.tile(np.asarray(idx).reshape(-1, 16).T, (8, 1)).astype(np.uint16)


def unstriped(offs):
    return offs[:16].T.reshape(-1).astype(np.int64)


E2M1 = np.array([0.0, 0.5, 1.0, 1.5, 2.0, 3.0, 4.0, 6.0, -0.0, -0.5, -1.0, -1.5, -2.0, -3.0, -4.0, -6.0])


def pack_weight(w, fmt):
    k, n = w.shape
    w = f64(np.asarray(w, np.float32).astype(ml_dtypes.bfloat16)).reshape(k // 32, 32, n)
    amax = np.abs(w).max(1)
    if fmt == "e4m3":
        byte = np.frexp(amax)[1] - 1 + 127 - 7
    else:
        mant, ex = np.frexp(amax / 6.0)
        byte = np.where(mant > 0.5, ex, ex - 1) + 127
    byte = np.clip(np.where(amax > 0, byte, 1), 1, 254)
    scaled = (w * np.exp2(127.0 - byte)[:, None, :]).reshape(k, n).astype(np.float32)
    by_word = np.ascontiguousarray(scaled.reshape(k // 512, 128, 4, n).transpose(0, 1, 3, 2))
    if fmt == "e4m3":
        words = by_word.astype(ml_dtypes.float8_e4m3fn).view(np.uint8)
    else:
        c = by_word.astype(ml_dtypes.float4_e2m1fn).view(np.uint8) & 0xF
        words = (c[..., 0::2] | (c[..., 1::2] << 4)).reshape(k // 512, 128, 2 * n)
    return np.ascontiguousarray(words), np.ascontiguousarray(byte.astype(np.uint8).reshape(k // 512, 16, n))


def unpack_weight(words, scales, fmt):
    g, _, n = scales.shape
    words = np.ascontiguousarray(words).reshape(g, 128, n, -1)
    if fmt == "e4m3":
        vals = words.view(ml_dtypes.float8_e4m3fn).astype(np.float64)
    else:
        nib = np.empty((g, 128, n, 4), np.uint8)
        nib[..., 0::2] = words & 0xF
        nib[..., 1::2] = words >> 4
        vals = E2M1[nib]
    vals = vals * np.repeat(np.exp2(scales.astype(np.float64) - 127.0), 8, axis=1)[..., None]
    return vals.transpose(0, 1, 3, 2).reshape(g * 512, n)


B, N, T, D, NQ = 1, 512, 2048, 1024, 128


def setup_inputs():
    n = np.random.standard_normal
    idx = np.random.permutation(T)[:B * N]
    idx2 = np.random.permutation(1024)[:B * N]
    s = mx_kscale(D)[:, None]
    kp = pack_weight(n((D, T)) / s, "e2m1")
    cp = pack_weight(n((D, 1024)) / s, "e2m1")
    return {
        "qT": (n((B, D, NQ)) * s * (1.00 / np.sqrt(D))).astype(np.float32),
        "k_words": np.ascontiguousarray(kp[0].reshape(1, 2, 128, T, 2).transpose(0, 2, 3, 1, 4)).reshape(1, 128, T, 4),
        "k_scales": kp[1],
        "c_words": np.ascontiguousarray(cp[0].reshape(1, 2, 128, 1024, 2).transpose(0, 2, 3, 1, 4)).reshape(1, 128, 1024, 4),
        "c_scales": cp[1],
        "offs": striped(idx),
        "offs2": striped(idx2),
    }


def reference(qT, k_words, k_scales, c_words, c_scales, offs, offs2):
    idx = unstriped(offs)
    idx2 = unstriped(offs2)
    pick = lambda x, which: x[:, which].reshape(x.shape[0], B, -1).transpose(1, 0, 2)
    k = unpack_weight(k_words.reshape(1, 128, T, 2, 2).transpose(0, 3, 1, 2, 4).reshape(2, 128, 2 * T), k_scales, "e2m1")
    kg = pick(k, idx)
    c = unpack_weight(c_words.reshape(1, 128, 1024, 2, 2).transpose(0, 3, 1, 2, 4).reshape(2, 128, 2 * 1024), c_scales, "e2m1")
    cg = pick(c, idx2)
    qq = mxq(f64(qT), 1, "e4m3")
    a = qq.transpose(0, 2, 1) @ kg
    z = qq.transpose(0, 2, 1) @ cg
    m = np.max(a, axis=-1, keepdims=True)
    e = np.exp(a - m)
    m2 = np.max(z, axis=-1, keepdims=True)
    e2 = np.exp(z - m2)
    y = e / np.sum(e, axis=-1, keepdims=True) + e2 / np.sum(e2, axis=-1, keepdims=True)
    return y

@@ -1,0 +1,155 @@
+from contextlib import ExitStack
+
+import concourse.mybir as mybir
+
+F32 = mybir.dt.float32
+BF16 = mybir.dt.bfloat16
+I32 = mybir.dt.int32
+U32 = mybir.dt.uint32
+U16 = mybir.dt.uint16
+U8 = mybir.dt.uint8
+FP8X4 = mybir.dt.float8_e4m3fn_x4
+FP4X4 = mybir.dt.float4_e2m1fn_x4
+ALU = mybir.AluOpType
+ACT = mybir.ActivationFunctionType
+AX = mybir.AxisListType
+
+P = 128
+NQ = 128
+N = 512
+D = 1024
+PASSES = 2
+SHIFT = 16
+
+FLOPS = 2 * 2 * NQ * N * D
+
+
+def tile_attend_sumw_topk_kernel(tc, qT, k_words, k_scales, c_words, c_scales, offs, offs2, out):
+    nc = tc.nc
+    with ExitStack() as ctx:
+        sb = ctx.enter_context(tc.tile_pool(name="sb", bufs=1))
+        placed = ctx.enter_context(tc.tile_pool(name="placed", bufs=1))
+        ps = ctx.enter_context(tc.psum_pool(name="ps", bufs=1))
+
+        warm_in = sb.tile([P, 1], F32)
+        warm_out = sb.tile([P, 1], F32)
+        zero_c = placed.tile([P, N // 4], I32, offset=4096 - 256, align_bytes=64)
+        zero_k = sb.tile([P, N // 4], I32, tag="k_wwin", align_bytes=64)
+        q_bf = sb.tile([P, PASSES, NQ, 4], BF16, align_bytes=64)
+        tables = {}
+        for name, words, scales, lst in (("c", c_words, c_scales, offs2), ("k", k_words, k_scales, offs)):
+            t = words.shape[2]
+            tables[name] = dict(
+                words=words,
+                scales=scales,
+                lst=lst,
+                offsets=sb.tile([P, N // 16], U16, name=name + "_offsets"),
+                wwin=(
+                    placed.tile([P, t], I32, name="c_wwin", offset=0, align_bytes=64)
+                    if name == "c"
+                    else sb.tile([P, t], I32, name="k_wwin", tag="k_wwin", align_bytes=64)
+                ),
+                swin=sb.tile([P, t], U8, name=name + "_swin", tag=name + "_swin", align_bytes=64),
+                gw=sb.tile([P, N], U32, name=name + "_gw", align_bytes=64),
+                gs=sb.tile([P, N], U8, name=name + "_gs", align_bytes=64),
+                s1=sb.tile([P, N], U8, name=name + "_s1", align_bytes=64),
+                w=[sb.tile([P, 2 * N], U8, name=name + "_w%d" % o, tag=name + "_w%d" % o, align_bytes=64) for o in range(PASSES)],
+                acc=ps.tile([P, N], F32, name=name + "_acc"),
+                e=sb.tile([P, N], F32, name=name + "_e", align_bytes=64),
+                total=sb.tile([P, 1], F32, name=name + "_total"),
+            )
+        c, k = tables["c"], tables["k"]
+        q_raw = placed.tile([P, PASSES, 4, NQ], F32, offset=4096, align_bytes=64)
+        q_codes = sb.tile([P, PASSES * NQ], U32, align_bytes=64)
+        q_scales = sb.tile([P, PASSES * NQ], U8, align_bytes=64)
+        part = sb.tile([P, N], F32, align_bytes=64)
+
+        nc.vector.memset(c["swin"][:].bitcast(I32), 0)
+        nc.vector.memset(zero_c[:], 0)
+        nc.vector.tensor_copy(c["s1"][:].bitcast(I32), zero_c[:])
+        nc.vector.memset(k["swin"][:].bitcast(I32), 0)
+        nc.vector.memset(zero_k[:], 0)
+        nc.vector.tensor_copy(k["s1"][:].bitcast(I32), zero_k[:])
+        nc.gpsimd.memset(warm_in[:], 0.0)
+        nc.scalar.activation(warm_out[:], warm_in[:], ACT.Exp)
+
+        def load_words(t):
+            nc.sync.dma_start(t["wwin"][:], t["words"][0].rearrange("p t b -> p (t b)").bitcast(I32))
+
+        def load_scales(t):
+            rows = t["scales"].rearrange("o (q j) t -> j q o t", j=4)
+            for j in range(4):
+                nc.sync.dma_start(t["swin"][j:P:SHIFT, :].bitcast(I32), rows[j].bitcast(I32))
+
+        nc.sync.dma_start(c["offsets"][:], c["lst"])
+        nc.sync.dma_start(k["offsets"][:], k["lst"])
+        load_scales(c)
+        load_words(c)
+        nc.sync.dma_start(
+            q_raw[:].rearrange("p o t m -> p o (t m)"),
+            qT[0].rearrange("(o p t) m -> p o (t m)", o=PASSES, t=4),
+        )
+        load_scales(k)
+        load_words(k)
+
+        def gather_words(t):
+            nc.vector.tensor_copy(t["gw"][:], t["wwin"][:].bitcast(U32).indirect(t["offsets"][:]))
+
+        def split_words(t):
+            halves = t["gw"][:].bitcast(U16).rearrange("p (n h) -> p h n", h=2)
+            for o in range(PASSES):
+                nc.vector.tensor_copy(t["w"][o][:].bitcast(U16), halves[:, o, :])
+
+        def gather_scales(t):
+            nc.vector.tensor_copy(t["gs"][:], t["swin"][:].indirect(t["offsets"][:]))
+            for lo, hi in ((0, 64), (64, 96), (96, 112)):
+                nc.sync.dma_start(t["s1"][lo:hi, :].bitcast(I32), t["gs"][lo + SHIFT : hi + SHIFT, :].bitcast(I32))
+
+        def scores(t):
+            planes = (t["gs"], t["s1"])
+            for o in range(PASSES):
+                cols = slice(o * NQ, (o + 1) * NQ)
+                nc.tensor.matmul_mx(
+                    out=t["acc"][:],
+                    lhsT=q_codes[:, cols].bitcast(FP8X4),
+                    lhsT_scale=q_scales[:, cols],
+                    rhs=t["w"][o][:].bitcast(FP4X4),
+                    rhs_scale=planes[o][:],
+                    start=(o == 0),
+                    stop=(o == PASSES - 1),
+                )
+
+        def softmax_terms(t, slot):
+            t["nmax"] = sb.tile([P, 1], F32, name=slot + "_nmax", tag=slot, align_bytes=64)
+            nc.vector.tensor_reduce(t["nmax"][:], t["acc"][:], AX.X, ALU.max, negate=True)
+            nc.scalar.activation(t["e"][:], t["acc"][:], ACT.Exp, bias=t["nmax"][:], accum_out=t["total"][:])
+
+        def invert(t, slot):
+            t["inv"] = sb.tile([P, 1], F32, name=slot + "_inv", tag=slot, align_bytes=64)
+            nc.vector.reciprocal(t["inv"][:], t["total"][:])
+
+        gather_scales(c)
+        gather_words(c)
+        gather_scales(k)
+        split_words(c)
+        for o in range(PASSES):
+            nc.scalar.copy(q_bf[:, o], q_raw[:, o].rearrange("p t m -> p m t"))
+        nc.vector.quantize_mx(
+            out=q_codes[:].bitcast(FP8X4),
+            scales=q_scales[:],
+            in_=q_bf[:].rearrange("p o m t -> p (o m t)"),
+        )
+        scores(c)
+        gather_words(k)
+        split_words(k)
+        scores(k)
+        softmax_terms(c, "k_wwin")
+        softmax_terms(k, "k_nmax")
+        invert(c, "k_w1")
+        nc.vector.tensor_scalar(part[:], c["e"][:], c["inv"][:], None, ALU.mult)
+        invert(k, "k_inv")
+        for h in range(2):
+            cols = slice(h * N // 2, (h + 1) * N // 2)
+            res = sb.tile([P, N // 2], F32, name="res%d" % h, align_bytes=64)
+            nc.vector.scalar_tensor_tensor(res[:], k["e"][:, cols], k["inv"][:], part[:, cols], ALU.mult, ALU.add)
+            nc.sync.dma_start(out[0][:, cols], res[:])

@@ -32,9 +32,8 @@ def tile_attend_sumw_topk_kernel(tc, qT, k_words, k_scales, c_words, c_scales, o
         ps = ctx.enter_context(tc.psum_pool(name="ps", bufs=1))
 
         warm_in = sb.tile([P, 1], F32)
-        warm_out = sb.tile([P, 1], F32)
+        warm_out = sb.tile([P, 1], F32, tag="k_wwin", align_bytes=64)
         zero_c = placed.tile([P, N // 4], I32, offset=4096 - 256, align_bytes=64)
-        zero_k = sb.tile([P, N // 4], I32, tag="k_wwin", align_bytes=64)
         q_bf = sb.tile([P, PASSES, NQ, 4], BF16, align_bytes=64)
         tables = {}
         for name, words, scales, lst in (("c", c_words, c_scales, offs2), ("k", k_words, k_scales, offs)):
@@ -49,18 +48,21 @@ def tile_attend_sumw_topk_kernel(tc, qT, k_words, k_scales, c_words, c_scales, o
                     if name == "c"
                     else sb.tile([P, t], I32, name="k_wwin", tag="k_wwin", align_bytes=64)
                 ),
-                swin=sb.tile([P, t], U8, name=name + "_swin", tag=name + "_swin", align_bytes=64),
+                swin=(
+                    sb.tile([P, t], U8, name="c_swin", align_bytes=64)
+                    if name == "c"
+                    else placed.tile([P, t], U8, name="k_swin", offset=8192 + 512, align_bytes=64)
+                ),
                 gw=sb.tile([P, N], U32, name=name + "_gw", align_bytes=64),
                 gs=sb.tile([P, N], U8, name=name + "_gs", align_bytes=64),
                 s1=sb.tile([P, N], U8, name=name + "_s1", align_bytes=64),
-                w=[sb.tile([P, 2 * N], U8, name=name + "_w%d" % o, tag=name + "_w%d" % o, align_bytes=64) for o in range(PASSES)],
                 acc=ps.tile([P, N], F32, name=name + "_acc"),
                 e=sb.tile([P, N], F32, name=name + "_e", align_bytes=64),
                 total=sb.tile([P, 1], F32, name=name + "_total"),
             )
         c, k = tables["c"], tables["k"]
         q_raw = placed.tile([P, PASSES, 4, NQ], F32, offset=4096, align_bytes=64)
-        q_codes = sb.tile([P, PASSES * NQ], U32, align_bytes=64)
+        q_codes = placed.tile([P, PASSES * NQ], U32, offset=8192, align_bytes=64)
         q_scales = sb.tile([P, PASSES * NQ], U8, align_bytes=64)
         part = sb.tile([P, N], F32, align_bytes=64)
 
@@ -68,8 +70,7 @@ def tile_attend_sumw_topk_kernel(tc, qT, k_words, k_scales, c_words, c_scales, o
         nc.vector.memset(zero_c[:], 0)
         nc.vector.tensor_copy(c["s1"][:].bitcast(I32), zero_c[:])
         nc.vector.memset(k["swin"][:].bitcast(I32), 0)
-        nc.vector.memset(zero_k[:], 0)
-        nc.vector.tensor_copy(k["s1"][:].bitcast(I32), zero_k[:])
+        nc.vector.memset(k["s1"][:].bitcast(I32), 0)
         nc.gpsimd.memset(warm_in[:], 0.0)
         nc.scalar.activation(warm_out[:], warm_in[:], ACT.Exp)
 
@@ -95,8 +96,11 @@ def tile_attend_sumw_topk_kernel(tc, qT, k_words, k_scales, c_words, c_scales, o
         def gather_words(t):
             nc.vector.tensor_copy(t["gw"][:], t["wwin"][:].bitcast(U32).indirect(t["offsets"][:]))
 
-        def split_words(t):
+        def split_words(t, places):
             halves = t["gw"][:].bitcast(U16).rearrange("p (n h) -> p h n", h=2)
+            t["w"] = [
+                placed.tile([P, 2 * N], U8, name="w%d_%d" % (places[0], at), offset=at, align_bytes=64) for at in places
+            ]
             for o in range(PASSES):
                 nc.vector.tensor_copy(t["w"][o][:].bitcast(U16), halves[:, o, :])
 
@@ -125,29 +129,32 @@ def tile_attend_sumw_topk_kernel(tc, qT, k_words, k_scales, c_words, c_scales, o
             nc.scalar.activation(t["e"][:], t["acc"][:], ACT.Exp, bias=t["nmax"][:], accum_out=t["total"][:])
 
         def invert(t, slot):
-            t["inv"] = sb.tile([P, 1], F32, name=slot + "_inv", tag=slot, align_bytes=64)
+            t["inv"] = placed.tile([P, 1], F32, name="inv%d" % slot, offset=slot, align_bytes=64)
             nc.vector.reciprocal(t["inv"][:], t["total"][:])
 
         gather_scales(c)
         gather_words(c)
         gather_scales(k)
-        split_words(c)
         for o in range(PASSES):
-            nc.scalar.copy(q_bf[:, o], q_raw[:, o].rearrange("p t m -> p m t"))
+            nc.scalar.copy(
+                q_bf[:, o].rearrange("p (m i) t -> p m t i", i=4),
+                q_raw[:, o].rearrange("p t (m i) -> p m t i", i=4),
+            )
         nc.vector.quantize_mx(
             out=q_codes[:].bitcast(FP8X4),
             scales=q_scales[:],
             in_=q_bf[:].rearrange("p o m t -> p (o m t)"),
         )
+        split_words(c, (9216, 10240))
         scores(c)
         gather_words(k)
-        split_words(k)
+        split_words(k, (10240, 11264))
         scores(k)
         softmax_terms(c, "k_wwin")
         softmax_terms(k, "k_nmax")
-        invert(c, "k_w1")
+        invert(c, 11264)
         nc.vector.tensor_scalar(part[:], c["e"][:], c["inv"][:], None, ALU.mult)
-        invert(k, "k_inv")
+        invert(k, 12288)
         for h in range(2):
             cols = slice(h * N // 2, (h + 1) * N // 2)
             res = sb.tile([P, N // 2], F32, name="res%d" % h, align_bytes=64)

@@ -66,31 +66,31 @@ def tile_attend_sumw_topk_kernel(tc, qT, k_words, k_scales, c_words, c_scales, o
         q_scales = sb.tile([P, PASSES * NQ], U8, align_bytes=64)
         part = sb.tile([P, N], F32, align_bytes=64)
 
+        nc.gpsimd.memset(zero_c[:], 0)
         nc.vector.memset(c["swin"][:].bitcast(I32), 0)
-        nc.vector.memset(zero_c[:], 0)
         nc.vector.tensor_copy(c["s1"][:].bitcast(I32), zero_c[:])
+        nc.vector.memset(warm_in[:], 0.0)
         nc.vector.memset(k["swin"][:].bitcast(I32), 0)
         nc.vector.memset(k["s1"][:].bitcast(I32), 0)
-        nc.gpsimd.memset(warm_in[:], 0.0)
-        nc.scalar.activation(warm_out[:], warm_in[:], ACT.Exp)
 
         def load_words(t):
             nc.sync.dma_start(t["wwin"][:], t["words"][0].rearrange("p t b -> p (t b)").bitcast(I32))
 
-        def load_scales(t):
+        def load_scales(t, queues):
             rows = t["scales"].rearrange("o (q j) t -> j q o t", j=4)
             for j in range(4):
-                nc.sync.dma_start(t["swin"][j:P:SHIFT, :].bitcast(I32), rows[j].bitcast(I32))
+                queues[j].dma_start(t["swin"][j:P:SHIFT, :].bitcast(I32), rows[j].bitcast(I32))
 
         nc.sync.dma_start(c["offsets"][:], c["lst"])
         nc.sync.dma_start(k["offsets"][:], k["lst"])
-        load_scales(c)
+        load_scales(c, (nc.sync, nc.scalar, nc.sync, nc.scalar))
+        nc.scalar.activation(warm_out[:], warm_in[:], ACT.Exp)
         load_words(c)
         nc.sync.dma_start(
             q_raw[:].rearrange("p o t m -> p o (t m)"),
             qT[0].rearrange("(o p t) m -> p o (t m)", o=PASSES, t=4),
         )
-        load_scales(k)
+        load_scales(k, (nc.sync,) * 4)
         load_words(k)
 
         def gather_words(t):

@@ -32,7 +32,8 @@ def tile_attend_sumw_topk_kernel(tc, qT, k_words, k_scales, c_words, c_scales, o
         ps = ctx.enter_context(tc.psum_pool(name="ps", bufs=1))
 
         warm_in = sb.tile([P, 1], F32)
-        warm_out = sb.tile([P, 1], F32, tag="k_wwin", align_bytes=64)
+        warm_out = sb.tile([P, 1], F32)
+        zero_k = sb.tile([P, N // 4], I32, tag="k_wwin", align_bytes=64)
         zero_c = placed.tile([P, N // 4], I32, offset=4096 - 256, align_bytes=64)
         q_bf = sb.tile([P, PASSES, NQ, 4], BF16, align_bytes=64)
         tables = {}
@@ -71,7 +72,8 @@ def tile_attend_sumw_topk_kernel(tc, qT, k_words, k_scales, c_words, c_scales, o
         nc.vector.tensor_copy(c["s1"][:].bitcast(I32), zero_c[:])
         nc.vector.memset(warm_in[:], 0.0)
         nc.vector.memset(k["swin"][:].bitcast(I32), 0)
-        nc.vector.memset(k["s1"][:].bitcast(I32), 0)
+        nc.vector.memset(zero_k[:], 0)
+        nc.vector.tensor_copy(k["s1"][:].bitcast(I32), zero_k[:])
 
         def load_words(t):
             nc.sync.dma_start(t["wwin"][:], t["words"][0].rearrange("p t b -> p (t b)").bitcast(I32))
@@ -147,12 +149,29 @@ def tile_attend_sumw_topk_kernel(tc, qT, k_words, k_scales, c_words, c_scales, o
         )
         split_words(c, (9216, 10240))
         scores(c)
-        gather_words(k)
-        split_words(k, (10240, 11264))
-        scores(k)
+        half = N // 2
+        got = [sb.tile([P, half], U32, name="k_got%d" % h, align_bytes=64) for h in range(2)]
+        for h in range(2):
+            lst = k["offsets"][:, h * half // 16 : (h + 1) * half // 16]
+            nc.vector.tensor_copy(got[h][:], k["wwin"][:].bitcast(U32).indirect(lst))
+        for g in range(4):
+            cols = slice(g * 128, (g + 1) * 128)
+            pair = placed.tile([P, PASSES, 256], U8, name="k_pair%d" % g, offset=10240 + 512 * g, align_bytes=64)
+            words = got[g // 2][:, (g % 2) * 128 : (g % 2 + 1) * 128]
+            nc.vector.tensor_copy(pair[:].bitcast(U16), words.bitcast(U16).rearrange("p (n o) -> p o n", o=2))
+            for o, plane in enumerate((k["gs"], k["s1"])):
+                nc.tensor.matmul_mx(
+                    out=k["acc"][:, cols],
+                    lhsT=q_codes[:, o * NQ : (o + 1) * NQ].bitcast(FP8X4),
+                    lhsT_scale=q_scales[:, o * NQ : (o + 1) * NQ],
+                    rhs=pair[:, o, :].bitcast(FP4X4),
+                    rhs_scale=plane[:, cols],
+                    start=(o == 0),
+                    stop=(o == PASSES - 1),
+                )
         softmax_terms(c, "k_wwin")
         softmax_terms(k, "k_nmax")
-        invert(c, 11264)
+        invert(c, 10240 + 512 * 3)
         nc.vector.tensor_scalar(part[:], c["e"][:], c["inv"][:], None, ALU.mult)
         invert(k, 12288)
         for h in range(2):

@@ -19,7 +19,7 @@ NQ = 128
 N = 512
 D = 1024
 PASSES = 2
-SHIFT = 16
+GROUP = 128
 
 FLOPS = 2 * 2 * NQ * N * D
 
@@ -28,102 +28,73 @@ def tile_attend_sumw_topk_kernel(tc, qT, k_words, k_scales, c_words, c_scales, o
     nc = tc.nc
     with ExitStack() as ctx:
         sb = ctx.enter_context(tc.tile_pool(name="sb", bufs=1))
-        placed = ctx.enter_context(tc.tile_pool(name="placed", bufs=1))
         ps = ctx.enter_context(tc.psum_pool(name="ps", bufs=1))
 
-        warm_in = sb.tile([P, 1], F32)
-        warm_out = sb.tile([P, 1], F32)
-        zero_k = sb.tile([P, N // 4], I32, tag="k_wwin", align_bytes=64)
-        zero_c = placed.tile([P, N // 4], I32, offset=4096 - 256, align_bytes=64)
-        q_bf = sb.tile([P, PASSES, NQ, 4], BF16, align_bytes=64)
         tables = {}
-        for name, words, scales, lst in (("c", c_words, c_scales, offs2), ("k", k_words, k_scales, offs)):
+        for name, words, scales, lst, base in (("c", c_words, c_scales, offs2, 48), ("k", k_words, k_scales, offs, 48)):
             t = words.shape[2]
             tables[name] = dict(
                 words=words,
                 scales=scales,
                 lst=lst,
+                base=base,
                 offsets=sb.tile([P, N // 16], U16, name=name + "_offsets"),
-                wwin=(
-                    placed.tile([P, t], I32, name="c_wwin", offset=0, align_bytes=64)
-                    if name == "c"
-                    else sb.tile([P, t], I32, name="k_wwin", tag="k_wwin", align_bytes=64)
-                ),
-                swin=(
-                    sb.tile([P, t], U8, name="c_swin", align_bytes=64)
-                    if name == "c"
-                    else placed.tile([P, t], U8, name="k_swin", offset=8192 + 512, align_bytes=64)
-                ),
-                gw=sb.tile([P, N], U32, name=name + "_gw", align_bytes=64),
+                wwin=sb.tile([P, t], I32, name=name + "_wwin", tag=name + "_wwin", align_bytes=64),
+                swin=sb.tile([P, t], U8, name=name + "_swin", align_bytes=64),
                 gs=sb.tile([P, N], U8, name=name + "_gs", align_bytes=64),
-                s1=sb.tile([P, N], U8, name=name + "_s1", align_bytes=64),
+                planes=[sb.tile([P, N], U8, name=name + "_plane%d" % o, align_bytes=64) for o in range(PASSES)],
                 acc=ps.tile([P, N], F32, name=name + "_acc"),
                 e=sb.tile([P, N], F32, name=name + "_e", align_bytes=64),
                 total=sb.tile([P, 1], F32, name=name + "_total"),
             )
         c, k = tables["c"], tables["k"]
-        q_raw = placed.tile([P, PASSES, 4, NQ], F32, offset=4096, align_bytes=64)
-        q_codes = placed.tile([P, PASSES * NQ], U32, offset=8192, align_bytes=64)
+        q_raw = sb.tile([P, PASSES, 4, NQ], F32, align_bytes=64)
+        q_bf = sb.tile([P, PASSES, NQ, 4], BF16, tag="k_got0", align_bytes=64)
+        q_codes = sb.tile([P, PASSES * NQ], U32, align_bytes=64)
         q_scales = sb.tile([P, PASSES * NQ], U8, align_bytes=64)
         part = sb.tile([P, N], F32, align_bytes=64)
-
-        nc.gpsimd.memset(zero_c[:], 0)
-        nc.vector.memset(c["swin"][:].bitcast(I32), 0)
-        nc.vector.tensor_copy(c["s1"][:].bitcast(I32), zero_c[:])
-        nc.vector.memset(warm_in[:], 0.0)
-        nc.vector.memset(k["swin"][:].bitcast(I32), 0)
-        nc.vector.memset(zero_k[:], 0)
-        nc.vector.tensor_copy(k["s1"][:].bitcast(I32), zero_k[:])
 
         def load_words(t):
             nc.sync.dma_start(t["wwin"][:], t["words"][0].rearrange("p t b -> p (t b)").bitcast(I32))
 
-        def load_scales(t, queues):
-            rows = t["scales"].rearrange("o (q j) t -> j q o t", j=4)
-            for j in range(4):
-                queues[j].dma_start(t["swin"][j:P:SHIFT, :].bitcast(I32), rows[j].bitcast(I32))
+        def load_scales(t, queue):
+            rows = t["scales"].rearrange("o (h u j) t -> u (o h) j t", h=2, u=2)
+            for u in range(2):
+                at = t["base"] + 32 * u
+                queue.dma_start(t["swin"][at : at + 16, :].bitcast(I32), rows[u].bitcast(I32))
 
-        nc.sync.dma_start(c["offsets"][:], c["lst"])
-        nc.sync.dma_start(k["offsets"][:], k["lst"])
-        load_scales(c, (nc.sync, nc.scalar, nc.sync, nc.scalar))
-        nc.scalar.activation(warm_out[:], warm_in[:], ACT.Exp)
+        for t, engine in ((c, nc.vector), (k, nc.gpsimd)):
+            for lo, hi in ((0, 48), (64, 80), (96, 128)):
+                engine.memset(t["swin"][lo:hi, :].bitcast(I32), 0)
+        for t in (c, k):
+            nc.sync.dma_start(t["offsets"][:], t["lst"])
+            load_scales(t, nc.sync)
         load_words(c)
         nc.sync.dma_start(
             q_raw[:].rearrange("p o t m -> p o (t m)"),
             qT[0].rearrange("(o p t) m -> p o (t m)", o=PASSES, t=4),
         )
-        load_scales(k, (nc.sync,) * 4)
         load_words(k)
-
-        def gather_words(t):
-            nc.vector.tensor_copy(t["gw"][:], t["wwin"][:].bitcast(U32).indirect(t["offsets"][:]))
-
-        def split_words(t, places):
-            halves = t["gw"][:].bitcast(U16).rearrange("p (n h) -> p h n", h=2)
-            t["w"] = [
-                placed.tile([P, 2 * N], U8, name="w%d_%d" % (places[0], at), offset=at, align_bytes=64) for at in places
-            ]
-            for o in range(PASSES):
-                nc.vector.tensor_copy(t["w"][o][:].bitcast(U16), halves[:, o, :])
 
         def gather_scales(t):
             nc.vector.tensor_copy(t["gs"][:], t["swin"][:].indirect(t["offsets"][:]))
-            for lo, hi in ((0, 64), (64, 96), (96, 112)):
-                nc.sync.dma_start(t["s1"][lo:hi, :].bitcast(I32), t["gs"][lo + SHIFT : hi + SHIFT, :].bitcast(I32))
-
-        def scores(t):
-            planes = (t["gs"], t["s1"])
             for o in range(PASSES):
-                cols = slice(o * NQ, (o + 1) * NQ)
-                nc.tensor.matmul_mx(
-                    out=t["acc"][:],
-                    lhsT=q_codes[:, cols].bitcast(FP8X4),
-                    lhsT_scale=q_scales[:, cols],
-                    rhs=t["w"][o][:].bitcast(FP4X4),
-                    rhs_scale=planes[o][:],
-                    start=(o == 0),
-                    stop=(o == PASSES - 1),
-                )
+                for h in range(2):
+                    at = t["base"] + 4 * (2 * o + h)
+                    nc.sync.dma_start(
+                        t["planes"][o][64 * h : 64 * h + 64, :].bitcast(I32), t["gs"][at : at + 64, :].bitcast(I32)
+                    )
+
+        def score_pass(t, o, cols, words):
+            nc.tensor.matmul_mx(
+                out=t["acc"][:, cols],
+                lhsT=q_codes[:, o * NQ : (o + 1) * NQ].bitcast(FP8X4),
+                lhsT_scale=q_scales[:, o * NQ : (o + 1) * NQ],
+                rhs=words.bitcast(FP4X4),
+                rhs_scale=t["planes"][o][:, cols],
+                start=(o == 0),
+                stop=(o == PASSES - 1),
+            )
 
         def softmax_terms(t, slot):
             t["nmax"] = sb.tile([P, 1], F32, name=slot + "_nmax", tag=slot, align_bytes=64)
@@ -131,12 +102,15 @@ def tile_attend_sumw_topk_kernel(tc, qT, k_words, k_scales, c_words, c_scales, o
             nc.scalar.activation(t["e"][:], t["acc"][:], ACT.Exp, bias=t["nmax"][:], accum_out=t["total"][:])
 
         def invert(t, slot):
-            t["inv"] = placed.tile([P, 1], F32, name="inv%d" % slot, offset=slot, align_bytes=64)
+            t["inv"] = sb.tile([P, 1], F32, name=slot + "_inv", tag=slot, align_bytes=64)
             nc.vector.reciprocal(t["inv"][:], t["total"][:])
 
         gather_scales(c)
-        gather_words(c)
         gather_scales(k)
+        c_got = sb.tile([P, N], U32, align_bytes=64)
+        nc.vector.tensor_copy(c_got[:], c["wwin"][:].bitcast(U32).indirect(c["offsets"][:]))
+        c_parted = sb.tile([P, PASSES, 2 * N], U8, align_bytes=64)
+        nc.vector.tensor_copy(c_parted[:].bitcast(U16), c_got[:].bitcast(U16).rearrange("p (n o) -> p o n", o=2))
         for o in range(PASSES):
             nc.scalar.copy(
                 q_bf[:, o].rearrange("p (m i) t -> p m t i", i=4),
@@ -147,33 +121,24 @@ def tile_attend_sumw_topk_kernel(tc, qT, k_words, k_scales, c_words, c_scales, o
             scales=q_scales[:],
             in_=q_bf[:].rearrange("p o m t -> p (o m t)"),
         )
-        split_words(c, (9216, 10240))
-        scores(c)
+        for o in range(PASSES):
+            score_pass(c, o, slice(0, N), c_parted[:, o, :])
         half = N // 2
-        got = [sb.tile([P, half], U32, name="k_got%d" % h, align_bytes=64) for h in range(2)]
+        got = [sb.tile([P, half], U32, name="k_got%d" % h, tag="k_got%d" % h, align_bytes=64) for h in range(2)]
         for h in range(2):
             lst = k["offsets"][:, h * half // 16 : (h + 1) * half // 16]
             nc.vector.tensor_copy(got[h][:], k["wwin"][:].bitcast(U32).indirect(lst))
-        for g in range(4):
-            cols = slice(g * 128, (g + 1) * 128)
-            pair = placed.tile([P, PASSES, 256], U8, name="k_pair%d" % g, offset=10240 + 512 * g, align_bytes=64)
-            words = got[g // 2][:, (g % 2) * 128 : (g % 2 + 1) * 128]
+        for g in range(N // GROUP):
+            pair = sb.tile([P, PASSES, 2 * GROUP], U8, name="k_pair%d" % g, tag="k_pair%d" % g, align_bytes=64)
+            words = got[g // 2][:, (g % 2) * GROUP : (g % 2 + 1) * GROUP]
             nc.vector.tensor_copy(pair[:].bitcast(U16), words.bitcast(U16).rearrange("p (n o) -> p o n", o=2))
-            for o, plane in enumerate((k["gs"], k["s1"])):
-                nc.tensor.matmul_mx(
-                    out=k["acc"][:, cols],
-                    lhsT=q_codes[:, o * NQ : (o + 1) * NQ].bitcast(FP8X4),
-                    lhsT_scale=q_scales[:, o * NQ : (o + 1) * NQ],
-                    rhs=pair[:, o, :].bitcast(FP4X4),
-                    rhs_scale=plane[:, cols],
-                    start=(o == 0),
-                    stop=(o == PASSES - 1),
-                )
+            for o in range(PASSES):
+                score_pass(k, o, slice(g * GROUP, (g + 1) * GROUP), pair[:, o, :])
         softmax_terms(c, "k_wwin")
         softmax_terms(k, "k_nmax")
-        invert(c, 10240 + 512 * 3)
+        invert(c, "k_pair3")
         nc.vector.tensor_scalar(part[:], c["e"][:], c["inv"][:], None, ALU.mult)
-        invert(k, 12288)
+        invert(k, "k_inv")
         for h in range(2):
             cols = slice(h * N // 2, (h + 1) * N // 2)
             res = sb.tile([P, N // 2], F32, name="res%d" % h, align_bytes=64)

@@ -31,27 +31,27 @@ def tile_attend_sumw_topk_kernel(tc, qT, k_words, k_scales, c_words, c_scales, o
         ps = ctx.enter_context(tc.psum_pool(name="ps", bufs=1))
 
         tables = {}
-        for name, words, scales, lst, base in (("c", c_words, c_scales, offs2, 48), ("k", k_words, k_scales, offs, 48)):
+        for name, words, scales, lst, first in (("c", c_words, c_scales, offs2, 0), ("k", k_words, k_scales, offs, N)):
             t = words.shape[2]
             tables[name] = dict(
                 words=words,
                 scales=scales,
                 lst=lst,
-                base=base,
                 offsets=sb.tile([P, N // 16], U16, name=name + "_offsets"),
                 wwin=sb.tile([P, t], I32, name=name + "_wwin", tag=name + "_wwin", align_bytes=64),
                 swin=sb.tile([P, t], U8, name=name + "_swin", align_bytes=64),
-                gs=sb.tile([P, N], U8, name=name + "_gs", align_bytes=64),
-                planes=[sb.tile([P, N], U8, name=name + "_plane%d" % o, align_bytes=64) for o in range(PASSES)],
+                first=first,
                 acc=ps.tile([P, N], F32, name=name + "_acc"),
                 e=sb.tile([P, N], F32, name=name + "_e", align_bytes=64),
                 total=sb.tile([P, 1], F32, name=name + "_total"),
             )
         c, k = tables["c"], tables["k"]
         q_raw = sb.tile([P, PASSES, 4, NQ], F32, align_bytes=64)
-        q_bf = sb.tile([P, PASSES, NQ, 4], BF16, tag="k_got0", align_bytes=64)
+        q_bf = sb.tile([P, PASSES, NQ, 4], BF16, tag="k_got", align_bytes=64)
         q_codes = sb.tile([P, PASSES * NQ], U32, align_bytes=64)
         q_scales = sb.tile([P, PASSES * NQ], U8, align_bytes=64)
+        got_scales = sb.tile([P, 2 * N], U8, align_bytes=64)
+        planes = [sb.tile([P, 2 * N], U8, name="plane%d" % o, align_bytes=64) for o in range(PASSES)]
         part = sb.tile([P, N], F32, align_bytes=64)
 
         def load_words(t):
@@ -60,11 +60,11 @@ def tile_attend_sumw_topk_kernel(tc, qT, k_words, k_scales, c_words, c_scales, o
         def load_scales(t, queue):
             rows = t["scales"].rearrange("o (h u j) t -> u (o h) j t", h=2, u=2)
             for u in range(2):
-                at = t["base"] + 32 * u
+                at = 48 + 32 * u
                 queue.dma_start(t["swin"][at : at + 16, :].bitcast(I32), rows[u].bitcast(I32))
 
-        for t, engine in ((c, nc.vector), (k, nc.gpsimd)):
-            for lo, hi in ((0, 48), (64, 80), (96, 128)):
+        for t, last in ((c, nc.vector), (k, nc.gpsimd)):
+            for engine, lo, hi in ((nc.vector, 0, 48), (nc.vector, 64, 80), (last, 96, 128)):
                 engine.memset(t["swin"][lo:hi, :].bitcast(I32), 0)
         for t in (c, k):
             nc.sync.dma_start(t["offsets"][:], t["lst"])
@@ -77,23 +77,17 @@ def tile_attend_sumw_topk_kernel(tc, qT, k_words, k_scales, c_words, c_scales, o
         load_words(k)
 
         def gather_scales(t):
-            nc.vector.tensor_copy(t["gs"][:], t["swin"][:].indirect(t["offsets"][:]))
-            for o in range(PASSES):
-                for h in range(2):
-                    at = t["base"] + 4 * (2 * o + h)
-                    nc.sync.dma_start(
-                        t["planes"][o][64 * h : 64 * h + 64, :].bitcast(I32), t["gs"][at : at + 64, :].bitcast(I32)
-                    )
+            nc.vector.tensor_copy(got_scales[:, t["first"] : t["first"] + N], t["swin"][:].indirect(t["offsets"][:]))
 
-        def score_pass(t, o, cols, words):
+        def score_pass(t, o, cols, words, first):
             nc.tensor.matmul_mx(
                 out=t["acc"][:, cols],
                 lhsT=q_codes[:, o * NQ : (o + 1) * NQ].bitcast(FP8X4),
                 lhsT_scale=q_scales[:, o * NQ : (o + 1) * NQ],
                 rhs=words.bitcast(FP4X4),
-                rhs_scale=t["planes"][o][:, cols],
-                start=(o == 0),
-                stop=(o == PASSES - 1),
+                rhs_scale=planes[o][:, t["first"] + cols.start : t["first"] + cols.stop],
+                start=first,
+                stop=not first,
             )
 
         def softmax_terms(t, slot):
@@ -107,6 +101,10 @@ def tile_attend_sumw_topk_kernel(tc, qT, k_words, k_scales, c_words, c_scales, o
 
         gather_scales(c)
         gather_scales(k)
+        for o in range(PASSES):
+            for h in range(2):
+                at = 48 + 4 * (2 * o + h)
+                nc.sync.dma_start(planes[o][64 * h : 64 * h + 64, :].bitcast(I32), got_scales[at : at + 64, :].bitcast(I32))
         c_got = sb.tile([P, N], U32, align_bytes=64)
         nc.vector.tensor_copy(c_got[:], c["wwin"][:].bitcast(U32).indirect(c["offsets"][:]))
         c_parted = sb.tile([P, PASSES, 2 * N], U8, align_bytes=64)
@@ -122,18 +120,18 @@ def tile_attend_sumw_topk_kernel(tc, qT, k_words, k_scales, c_words, c_scales, o
             in_=q_bf[:].rearrange("p o m t -> p (o m t)"),
         )
         for o in range(PASSES):
-            score_pass(c, o, slice(0, N), c_parted[:, o, :])
+            score_pass(c, o, slice(0, N), c_parted[:, o, :], o == 0)
         half = N // 2
-        got = [sb.tile([P, half], U32, name="k_got%d" % h, tag="k_got%d" % h, align_bytes=64) for h in range(2)]
+        k_got = sb.tile([P, N], U32, tag="k_got", align_bytes=64)
         for h in range(2):
             lst = k["offsets"][:, h * half // 16 : (h + 1) * half // 16]
-            nc.vector.tensor_copy(got[h][:], k["wwin"][:].bitcast(U32).indirect(lst))
+            nc.vector.tensor_copy(k_got[:, h * half : (h + 1) * half], k["wwin"][:].bitcast(U32).indirect(lst))
         for g in range(N // GROUP):
             pair = sb.tile([P, PASSES, 2 * GROUP], U8, name="k_pair%d" % g, tag="k_pair%d" % g, align_bytes=64)
-            words = got[g // 2][:, (g % 2) * GROUP : (g % 2 + 1) * GROUP]
+            words = k_got[:, g * GROUP : (g + 1) * GROUP]
             nc.vector.tensor_copy(pair[:].bitcast(U16), words.bitcast(U16).rearrange("p (n o) -> p o n", o=2))
-            for o in range(PASSES):
-                score_pass(k, o, slice(g * GROUP, (g + 1) * GROUP), pair[:, o, :])
+            for o in (1, 0):
+                score_pass(k, o, slice(g * GROUP, (g + 1) * GROUP), pair[:, o, :], o == 1)
         softmax_terms(c, "k_wwin")
         softmax_terms(k, "k_nmax")
         invert(c, "k_pair3")

@@ -46,7 +46,7 @@ def tile_attend_sumw_topk_kernel(tc, qT, k_words, k_scales, c_words, c_scales, o
                 total=sb.tile([P, 1], F32, name=name + "_total"),
             )
         c, k = tables["c"], tables["k"]
-        q_raw = sb.tile([P, PASSES, 4, NQ], F32, align_bytes=64)
+        q_raw = [sb.tile([P, 4, NQ], F32, name="q_raw%d" % o, tag="q_raw%d" % o, align_bytes=64) for o in range(PASSES)]
         q_bf = sb.tile([P, PASSES, NQ, 4], BF16, tag="k_got", align_bytes=64)
         q_codes = sb.tile([P, PASSES * NQ], U32, align_bytes=64)
         q_scales = sb.tile([P, PASSES * NQ], U8, align_bytes=64)
@@ -57,23 +57,22 @@ def tile_attend_sumw_topk_kernel(tc, qT, k_words, k_scales, c_words, c_scales, o
         def load_words(t):
             nc.sync.dma_start(t["wwin"][:], t["words"][0].rearrange("p t b -> p (t b)").bitcast(I32))
 
-        def load_scales(t, queue):
+        def load_scales(t, queues):
             rows = t["scales"].rearrange("o (h u j) t -> u (o h) j t", h=2, u=2)
             for u in range(2):
                 at = 48 + 32 * u
-                queue.dma_start(t["swin"][at : at + 16, :].bitcast(I32), rows[u].bitcast(I32))
+                queues[u].dma_start(t["swin"][at : at + 16, :].bitcast(I32), rows[u].bitcast(I32))
 
         for t, last in ((c, nc.vector), (k, nc.gpsimd)):
             for engine, lo, hi in ((nc.vector, 0, 48), (nc.vector, 64, 80), (last, 96, 128)):
                 engine.memset(t["swin"][lo:hi, :].bitcast(I32), 0)
-        for t in (c, k):
+        for t, queues in ((c, (nc.sync, nc.scalar)), (k, (nc.scalar, nc.scalar))):
             nc.sync.dma_start(t["offsets"][:], t["lst"])
-            load_scales(t, nc.sync)
+            load_scales(t, queues)
         load_words(c)
-        nc.sync.dma_start(
-            q_raw[:].rearrange("p o t m -> p o (t m)"),
-            qT[0].rearrange("(o p t) m -> p o (t m)", o=PASSES, t=4),
-        )
+        q_rows = qT[0].rearrange("(o p t) m -> o p (t m)", o=PASSES, t=4)
+        for o in range(PASSES):
+            nc.sync.dma_start(q_raw[o][:].rearrange("p t m -> p (t m)"), q_rows[o])
         load_words(k)
 
         def gather_scales(t):
@@ -107,18 +106,18 @@ def tile_attend_sumw_topk_kernel(tc, qT, k_words, k_scales, c_words, c_scales, o
                 nc.sync.dma_start(planes[o][64 * h : 64 * h + 64, :].bitcast(I32), got_scales[at : at + 64, :].bitcast(I32))
         c_got = sb.tile([P, N], U32, align_bytes=64)
         nc.vector.tensor_copy(c_got[:], c["wwin"][:].bitcast(U32).indirect(c["offsets"][:]))
-        c_parted = sb.tile([P, PASSES, 2 * N], U8, align_bytes=64)
-        nc.vector.tensor_copy(c_parted[:].bitcast(U16), c_got[:].bitcast(U16).rearrange("p (n o) -> p o n", o=2))
         for o in range(PASSES):
             nc.scalar.copy(
                 q_bf[:, o].rearrange("p (m i) t -> p m t i", i=4),
-                q_raw[:, o].rearrange("p t (m i) -> p m t i", i=4),
+                q_raw[o][:].rearrange("p t (m i) -> p m t i", i=4),
             )
         nc.vector.quantize_mx(
             out=q_codes[:].bitcast(FP8X4),
             scales=q_scales[:],
             in_=q_bf[:].rearrange("p o m t -> p (o m t)"),
         )
+        c_parted = sb.tile([P, PASSES, 2 * N], U8, tag="q_raw1", align_bytes=64)
+        nc.vector.tensor_copy(c_parted[:].bitcast(U16), c_got[:].bitcast(U16).rearrange("p (n o) -> p o n", o=2))
         for o in range(PASSES):
             score_pass(c, o, slice(0, N), c_parted[:, o, :], o == 0)
         half = N // 2

@@ -116,6 +116,16 @@ def tile_attend_sumw_topk_kernel(tc, qT, k_words, k_scales, c_words, c_scales, o
             scales=q_scales[:],
             in_=q_bf[:].rearrange("p o m t -> p (o m t)"),
         )
+        warm = ps.tile([P, N], F32)
+        nc.tensor.matmul_mx(
+            out=warm[:],
+            lhsT=q_codes[:, 0:NQ].bitcast(FP8X4),
+            lhsT_scale=q_scales[:, 0:NQ],
+            rhs=c_got[:, 0 : N // 2].bitcast(FP4X4),
+            rhs_scale=got_scales[:, 0:N],
+            start=True,
+            stop=True,
+        )
         c_parted = sb.tile([P, PASSES, 2 * N], U8, tag="q_raw1", align_bytes=64)
         nc.vector.tensor_copy(c_parted[:].bitcast(U16), c_got[:].bitcast(U16).rearrange("p (n o) -> p o n", o=2))
         for o in range(PASSES):

@@ -20,6 +20,7 @@ N = 512
 D = 1024
 PASSES = 2
 GROUP = 128
+ROWS = 32
 
 FLOPS = 2 * 2 * NQ * N * D
 
@@ -39,7 +40,7 @@ def tile_attend_sumw_topk_kernel(tc, qT, k_words, k_scales, c_words, c_scales, o
                 lst=lst,
                 offsets=sb.tile([P, N // 16], U16, name=name + "_offsets"),
                 wwin=sb.tile([P, t], I32, name=name + "_wwin", tag=name + "_wwin", align_bytes=64),
-                swin=sb.tile([P, t], U8, name=name + "_swin", align_bytes=64),
+                swin=sb.tile([P, t], U8, name=name + "_swin", tag=name + "_swin", align_bytes=64),
                 first=first,
                 acc=ps.tile([P, N], F32, name=name + "_acc"),
                 e=sb.tile([P, N], F32, name=name + "_e", align_bytes=64),
@@ -51,28 +52,22 @@ def tile_attend_sumw_topk_kernel(tc, qT, k_words, k_scales, c_words, c_scales, o
         q_codes = sb.tile([P, PASSES * NQ], U32, align_bytes=64)
         q_scales = sb.tile([P, PASSES * NQ], U8, align_bytes=64)
         got_scales = sb.tile([P, 2 * N], U8, align_bytes=64)
-        planes = [sb.tile([P, 2 * N], U8, name="plane%d" % o, align_bytes=64) for o in range(PASSES)]
         part = sb.tile([P, N], F32, align_bytes=64)
 
         def load_words(t):
-            nc.sync.dma_start(t["wwin"][:], t["words"][0].rearrange("p t b -> p (t b)").bitcast(I32))
+            nc.scalar.dma_start(t["wwin"][:], t["words"][0].rearrange("p t b -> p (t b)").bitcast(I32))
 
-        def load_scales(t, queues):
-            rows = t["scales"].rearrange("o (h u j) t -> u (o h) j t", h=2, u=2)
-            for u in range(2):
-                at = 48 + 32 * u
-                queues[u].dma_start(t["swin"][at : at + 16, :].bitcast(I32), rows[u].bitcast(I32))
-
-        for t, last in ((c, nc.vector), (k, nc.gpsimd)):
-            for engine, lo, hi in ((nc.vector, 0, 48), (nc.vector, 64, 80), (last, 96, 128)):
-                engine.memset(t["swin"][lo:hi, :].bitcast(I32), 0)
-        for t, queues in ((c, (nc.sync, nc.scalar)), (k, (nc.scalar, nc.scalar))):
+        for t in (c, k):
+            for lo, hi in ((32, 64), (64, 128)):
+                nc.vector.memset(t["swin"][lo:hi, :].bitcast(I32), 0)
+        for t in (c, k):
             nc.sync.dma_start(t["offsets"][:], t["lst"])
-            load_scales(t, queues)
+            rows = t["scales"].rearrange("o f t -> (o f) t")
+            nc.scalar.dma_start(t["swin"][0:ROWS, :].bitcast(I32), rows.bitcast(I32))
         load_words(c)
         q_rows = qT[0].rearrange("(o p t) m -> o p (t m)", o=PASSES, t=4)
         for o in range(PASSES):
-            nc.sync.dma_start(q_raw[o][:].rearrange("p t m -> p (t m)"), q_rows[o])
+            nc.scalar.dma_start(q_raw[o][:].rearrange("p t m -> p (t m)"), q_rows[o])
         load_words(k)
 
         def gather_scales(t):
@@ -101,16 +96,19 @@ def tile_attend_sumw_topk_kernel(tc, qT, k_words, k_scales, c_words, c_scales, o
         gather_scales(c)
         gather_scales(k)
         for o in range(PASSES):
-            for h in range(2):
-                at = 48 + 4 * (2 * o + h)
-                nc.sync.dma_start(planes[o][64 * h : 64 * h + 64, :].bitcast(I32), got_scales[at : at + 64, :].bitcast(I32))
-        c_got = sb.tile([P, N], U32, align_bytes=64)
-        nc.vector.tensor_copy(c_got[:], c["wwin"][:].bitcast(U32).indirect(c["offsets"][:]))
-        for o in range(PASSES):
             nc.scalar.copy(
                 q_bf[:, o].rearrange("p (m i) t -> p m t i", i=4),
                 q_raw[o][:].rearrange("p t (m i) -> p m t i", i=4),
             )
+        planes = [sb.tile([P, 2 * N], U8, name="plane%d" % o, tag=tag, align_bytes=64) for o, tag in enumerate(("q_raw0", "plane1"))]
+        for o in (1, 0):
+            for quad in range(4):
+                at = 16 * o + 4 * quad
+                if at > 0:
+                    nc.sync.dma_start(planes[o][32 * quad : 32 * quad + 4, :].bitcast(I32), got_scales[at : at + 4, :].bitcast(I32))
+        c_got = sb.tile([P, N], U32, align_bytes=64)
+        nc.vector.tensor_copy(c_got[:], c["wwin"][:].bitcast(U32).indirect(c["offsets"][:]))
+        nc.vector.tensor_copy(planes[0][0:4, :].bitcast(I32), got_scales[0:4, :].bitcast(I32))
         nc.vector.quantize_mx(
             out=q_codes[:].bitcast(FP8X4),
             scales=q_scales[:],
@@ -128,8 +126,8 @@ def tile_attend_sumw_topk_kernel(tc, qT, k_words, k_scales, c_words, c_scales, o
         )
         c_parted = sb.tile([P, PASSES, 2 * N], U8, tag="q_raw1", align_bytes=64)
         nc.vector.tensor_copy(c_parted[:].bitcast(U16), c_got[:].bitcast(U16).rearrange("p (n o) -> p o n", o=2))
-        for o in range(PASSES):
-            score_pass(c, o, slice(0, N), c_parted[:, o, :], o == 0)
+        for o in (1, 0):
+            score_pass(c, o, slice(0, N), c_parted[:, o, :], o == 1)
         half = N // 2
         k_got = sb.tile([P, N], U32, tag="k_got", align_bytes=64)
         for h in range(2):
@@ -139,8 +137,8 @@ def tile_attend_sumw_topk_kernel(tc, qT, k_words, k_scales, c_words, c_scales, o
             pair = sb.tile([P, PASSES, 2 * GROUP], U8, name="k_pair%d" % g, tag="k_pair%d" % g, align_bytes=64)
             words = k_got[:, g * GROUP : (g + 1) * GROUP]
             nc.vector.tensor_copy(pair[:].bitcast(U16), words.bitcast(U16).rearrange("p (n o) -> p o n", o=2))
-            for o in (1, 0):
-                score_pass(k, o, slice(g * GROUP, (g + 1) * GROUP), pair[:, o, :], o == 1)
+            for o in (0, 1):
+                score_pass(k, o, slice(g * GROUP, (g + 1) * GROUP), pair[:, o, :], o == 0)
         softmax_terms(c, "k_wwin")
         softmax_terms(k, "k_nmax")
         invert(c, "k_pair3")

@@ -29,6 +29,7 @@ def tile_attend_sumw_topk_kernel(tc, qT, k_words, k_scales, c_words, c_scales, o
     nc = tc.nc
     with ExitStack() as ctx:
         sb = ctx.enter_context(tc.tile_pool(name="sb", bufs=1))
+        placed = ctx.enter_context(tc.tile_pool(name="placed", bufs=1))
         ps = ctx.enter_context(tc.psum_pool(name="ps", bufs=1))
 
         tables = {}
@@ -47,8 +48,8 @@ def tile_attend_sumw_topk_kernel(tc, qT, k_words, k_scales, c_words, c_scales, o
                 total=sb.tile([P, 1], F32, name=name + "_total"),
             )
         c, k = tables["c"], tables["k"]
-        q_raw = [sb.tile([P, 4, NQ], F32, name="q_raw%d" % o, tag="q_raw%d" % o, align_bytes=64) for o in range(PASSES)]
-        q_bf = sb.tile([P, PASSES, NQ, 4], BF16, tag="k_got", align_bytes=64)
+        q_raw = [placed.tile([P, 4, NQ], F32, name="q_raw%d" % o, offset=2048 + 2560 * o, align_bytes=64) for o in range(PASSES)]
+        q_bf = [sb.tile([P, NQ, 4], BF16, name="q_bf%d" % o, tag="q_bf%d" % o, align_bytes=64) for o in range(PASSES)]
         q_codes = sb.tile([P, PASSES * NQ], U32, align_bytes=64)
         q_scales = sb.tile([P, PASSES * NQ], U8, align_bytes=64)
         got_scales = sb.tile([P, 2 * N], U8, align_bytes=64)
@@ -66,9 +67,9 @@ def tile_attend_sumw_topk_kernel(tc, qT, k_words, k_scales, c_words, c_scales, o
             nc.scalar.dma_start(t["swin"][0:ROWS, :].bitcast(I32), rows.bitcast(I32))
         load_words(c)
         q_rows = qT[0].rearrange("(o p t) m -> o p (t m)", o=PASSES, t=4)
-        for o in range(PASSES):
-            nc.scalar.dma_start(q_raw[o][:].rearrange("p t m -> p (t m)"), q_rows[o])
+        nc.scalar.dma_start(q_raw[0][:].rearrange("p t m -> p (t m)"), q_rows[0])
         load_words(k)
+        nc.scalar.dma_start(q_raw[1][:].rearrange("p t m -> p (t m)"), q_rows[1])
 
         def gather_scales(t):
             nc.vector.tensor_copy(got_scales[:, t["first"] : t["first"] + N], t["swin"][:].indirect(t["offsets"][:]))
@@ -89,31 +90,37 @@ def tile_attend_sumw_topk_kernel(tc, qT, k_words, k_scales, c_words, c_scales, o
             nc.vector.tensor_reduce(t["nmax"][:], t["acc"][:], AX.X, ALU.max, negate=True)
             nc.scalar.activation(t["e"][:], t["acc"][:], ACT.Exp, bias=t["nmax"][:], accum_out=t["total"][:])
 
-        def invert(t, slot):
-            t["inv"] = sb.tile([P, 1], F32, name=slot + "_inv", tag=slot, align_bytes=64)
+        def invert(t, inv):
+            t["inv"] = inv
             nc.vector.reciprocal(t["inv"][:], t["total"][:])
+
+        def cast_pass(o):
+            nc.scalar.copy(
+                q_bf[o][:].rearrange("p (m i) t -> p m t i", i=4),
+                q_raw[o][:].rearrange("p t (m i) -> p m t i", i=4),
+            )
+
+        def quantise_pass(o):
+            nc.vector.quantize_mx(
+                out=q_codes[:, o * NQ : (o + 1) * NQ].bitcast(FP8X4),
+                scales=q_scales[:, o * NQ : (o + 1) * NQ],
+                in_=q_bf[o][:].rearrange("p m t -> p (m t)"),
+            )
+
+        def part_words(parted, words):
+            nc.vector.tensor_copy(parted.bitcast(U16), words.bitcast(U16).rearrange("p (n o) -> p o n", o=2))
 
         gather_scales(c)
         gather_scales(k)
-        for o in range(PASSES):
-            nc.scalar.copy(
-                q_bf[:, o].rearrange("p (m i) t -> p m t i", i=4),
-                q_raw[o][:].rearrange("p t (m i) -> p m t i", i=4),
-            )
-        planes = [sb.tile([P, 2 * N], U8, name="plane%d" % o, tag=tag, align_bytes=64) for o, tag in enumerate(("q_raw0", "plane1"))]
-        for o in (1, 0):
-            for quad in range(4):
-                at = 16 * o + 4 * quad
-                if at > 0:
-                    nc.sync.dma_start(planes[o][32 * quad : 32 * quad + 4, :].bitcast(I32), got_scales[at : at + 4, :].bitcast(I32))
+        cast_pass(0)
+        planes = [placed.tile([P, 2 * N], U8, name="plane%d" % o, offset=2560 + 1024 * o, align_bytes=64) for o in range(PASSES)]
+        for at in range(4, ROWS, 4):
+            o, quad = divmod(at // 4, 4)
+            nc.sync.dma_start(planes[o][32 * quad : 32 * quad + 4, :].bitcast(I32), got_scales[at : at + 4, :].bitcast(I32))
         c_got = sb.tile([P, N], U32, align_bytes=64)
         nc.vector.tensor_copy(c_got[:], c["wwin"][:].bitcast(U32).indirect(c["offsets"][:]))
         nc.vector.tensor_copy(planes[0][0:4, :].bitcast(I32), got_scales[0:4, :].bitcast(I32))
-        nc.vector.quantize_mx(
-            out=q_codes[:].bitcast(FP8X4),
-            scales=q_scales[:],
-            in_=q_bf[:].rearrange("p o m t -> p (o m t)"),
-        )
+        quantise_pass(0)
         warm = ps.tile([P, N], F32)
         nc.tensor.matmul_mx(
             out=warm[:],
@@ -124,26 +131,28 @@ def tile_attend_sumw_topk_kernel(tc, qT, k_words, k_scales, c_words, c_scales, o
             start=True,
             stop=True,
         )
-        c_parted = sb.tile([P, PASSES, 2 * N], U8, tag="q_raw1", align_bytes=64)
-        nc.vector.tensor_copy(c_parted[:].bitcast(U16), c_got[:].bitcast(U16).rearrange("p (n o) -> p o n", o=2))
-        for o in (1, 0):
-            score_pass(c, o, slice(0, N), c_parted[:, o, :], o == 1)
+        c_parted = placed.tile([P, PASSES, 2 * N], U8, offset=512, align_bytes=64)
+        part_words(c_parted[:], c_got[:])
+        score_pass(c, 0, slice(0, N), c_parted[:, 0, :], True)
         half = N // 2
-        k_got = sb.tile([P, N], U32, tag="k_got", align_bytes=64)
+        k_got = sb.tile([P, N], U32, tag="q_bf0", align_bytes=64)
         for h in range(2):
             lst = k["offsets"][:, h * half // 16 : (h + 1) * half // 16]
             nc.vector.tensor_copy(k_got[:, h * half : (h + 1) * half], k["wwin"][:].bitcast(U32).indirect(lst))
+        cast_pass(1)
         for g in range(N // GROUP):
-            pair = sb.tile([P, PASSES, 2 * GROUP], U8, name="k_pair%d" % g, tag="k_pair%d" % g, align_bytes=64)
-            words = k_got[:, g * GROUP : (g + 1) * GROUP]
-            nc.vector.tensor_copy(pair[:].bitcast(U16), words.bitcast(U16).rearrange("p (n o) -> p o n", o=2))
-            for o in (0, 1):
-                score_pass(k, o, slice(g * GROUP, (g + 1) * GROUP), pair[:, o, :], o == 0)
+            pair = placed.tile([P, PASSES, 2 * GROUP], U8, name="k_pair%d" % g, offset=6656 - 4 * GROUP * g, align_bytes=64)
+            part_words(pair[:], k_got[:, g * GROUP : (g + 1) * GROUP])
+            if g == 0:
+                quantise_pass(1)
+                score_pass(c, 1, slice(0, N), c_parted[:, 1, :], False)
+            for o in (1, 0):
+                score_pass(k, o, slice(g * GROUP, (g + 1) * GROUP), pair[:, o, :], o == 1)
         softmax_terms(c, "k_wwin")
         softmax_terms(k, "k_nmax")
-        invert(c, "k_pair3")
+        invert(c, placed.tile([P, 1], F32, name="c_inv", offset=6656 - 4 * GROUP * 3, align_bytes=64))
         nc.vector.tensor_scalar(part[:], c["e"][:], c["inv"][:], None, ALU.mult)
-        invert(k, "k_inv")
+        invert(k, sb.tile([P, 1], F32, name="k_inv", align_bytes=64))
         for h in range(2):
             cols = slice(h * N // 2, (h + 1) * N // 2)
             res = sb.tile([P, N // 2], F32, name="res%d" % h, align_bytes=64)

@@ -33,7 +33,7 @@ def tile_attend_sumw_topk_kernel(tc, qT, k_words, k_scales, c_words, c_scales, o
         ps = ctx.enter_context(tc.psum_pool(name="ps", bufs=1))
 
         tables = {}
-        for name, words, scales, lst, first in (("c", c_words, c_scales, offs2, 0), ("k", k_words, k_scales, offs, N)):
+        for name, words, scales, lst, first, at in (("c", c_words, c_scales, offs2, 0, 4608), ("k", k_words, k_scales, offs, N, 7168)):
             t = words.shape[2]
             tables[name] = dict(
                 words=words,
@@ -41,22 +41,27 @@ def tile_attend_sumw_topk_kernel(tc, qT, k_words, k_scales, c_words, c_scales, o
                 lst=lst,
                 offsets=sb.tile([P, N // 16], U16, name=name + "_offsets"),
                 wwin=sb.tile([P, t], I32, name=name + "_wwin", tag=name + "_wwin", align_bytes=64),
-                swin=sb.tile([P, t], U8, name=name + "_swin", tag=name + "_swin", align_bytes=64),
+                swin=placed.tile([P, t], U8, name=name + "_swin", offset=at, align_bytes=64),
                 first=first,
                 acc=ps.tile([P, N], F32, name=name + "_acc"),
                 e=sb.tile([P, N], F32, name=name + "_e", align_bytes=64),
                 total=sb.tile([P, 1], F32, name=name + "_total"),
             )
         c, k = tables["c"], tables["k"]
-        q_raw = [placed.tile([P, 4, NQ], F32, name="q_raw%d" % o, offset=2048 + 2560 * o, align_bytes=64) for o in range(PASSES)]
+        q_raw = {}
         q_bf = [sb.tile([P, NQ, 4], BF16, name="q_bf%d" % o, tag="q_bf%d" % o, align_bytes=64) for o in range(PASSES)]
         q_codes = sb.tile([P, PASSES * NQ], U32, align_bytes=64)
         q_scales = sb.tile([P, PASSES * NQ], U8, align_bytes=64)
         got_scales = sb.tile([P, 2 * N], U8, align_bytes=64)
         part = sb.tile([P, N], F32, align_bytes=64)
 
+        def load_queries(o):
+            q_raw[o] = placed.tile([P, 4, NQ], F32, name="q_raw%d" % o, offset=(2048, 4608)[o], align_bytes=64)
+            rows = qT[0].rearrange("(o p t) m -> o p (t m)", o=PASSES, t=4)[o]
+            nc.sync.dma_start(q_raw[o][:].rearrange("p t m -> p (t m)"), rows)
+
         def load_words(t):
-            nc.scalar.dma_start(t["wwin"][:], t["words"][0].rearrange("p t b -> p (t b)").bitcast(I32))
+            nc.sync.dma_start(t["wwin"][:], t["words"][0].rearrange("p t b -> p (t b)").bitcast(I32))
 
         for t in (c, k):
             for lo, hi in ((32, 64), (64, 128)):
@@ -66,10 +71,8 @@ def tile_attend_sumw_topk_kernel(tc, qT, k_words, k_scales, c_words, c_scales, o
             rows = t["scales"].rearrange("o f t -> (o f) t")
             nc.scalar.dma_start(t["swin"][0:ROWS, :].bitcast(I32), rows.bitcast(I32))
         load_words(c)
-        q_rows = qT[0].rearrange("(o p t) m -> o p (t m)", o=PASSES, t=4)
-        nc.scalar.dma_start(q_raw[0][:].rearrange("p t m -> p (t m)"), q_rows[0])
+        load_queries(0)
         load_words(k)
-        nc.scalar.dma_start(q_raw[1][:].rearrange("p t m -> p (t m)"), q_rows[1])
 
         def gather_scales(t):
             nc.vector.tensor_copy(got_scales[:, t["first"] : t["first"] + N], t["swin"][:].indirect(t["offsets"][:]))
@@ -80,7 +83,7 @@ def tile_attend_sumw_topk_kernel(tc, qT, k_words, k_scales, c_words, c_scales, o
                 lhsT=q_codes[:, o * NQ : (o + 1) * NQ].bitcast(FP8X4),
                 lhsT_scale=q_scales[:, o * NQ : (o + 1) * NQ],
                 rhs=words.bitcast(FP4X4),
-                rhs_scale=planes[o][:, t["first"] + cols.start : t["first"] + cols.stop],
+                rhs_scale=t["planes"][o][:, cols],
                 start=first,
                 stop=not first,
             )
@@ -110,16 +113,29 @@ def tile_attend_sumw_topk_kernel(tc, qT, k_words, k_scales, c_words, c_scales, o
         def part_words(parted, words):
             nc.vector.tensor_copy(parted.bitcast(U16), words.bitcast(U16).rearrange("p (n o) -> p o n", o=2))
 
+        def move_rows(plane, o, quads, cols):
+            for quad in quads:
+                at = 16 * o + 4 * quad
+                nc.sync.dma_start(plane[32 * quad : 32 * quad + 4, :].bitcast(I32), got_scales[at : at + 4, cols].bitcast(I32))
+
+        def copy_rows(plane, cols):
+            nc.vector.tensor_copy(plane[0:4, :].bitcast(I32), got_scales[0:4, cols].bitcast(I32))
+
         gather_scales(c)
+        c_plane0 = sb.tile([P, N], U8, align_bytes=64)
+        move_rows(c_plane0, 0, range(4), slice(0, N))
+        load_queries(1)
         gather_scales(k)
+        plane1 = sb.tile([P, 2 * N], U8, align_bytes=64)
+        move_rows(plane1, 1, range(4), slice(0, 2 * N))
         cast_pass(0)
-        planes = [placed.tile([P, 2 * N], U8, name="plane%d" % o, offset=2560 + 1024 * o, align_bytes=64) for o in range(PASSES)]
-        for at in range(4, ROWS, 4):
-            o, quad = divmod(at // 4, 4)
-            nc.sync.dma_start(planes[o][32 * quad : 32 * quad + 4, :].bitcast(I32), got_scales[at : at + 4, :].bitcast(I32))
+        k_plane0 = placed.tile([P, N], U8, offset=1792, align_bytes=64)
+        move_rows(k_plane0, 0, (1, 2, 3), slice(N, 2 * N))
+        c["planes"] = (c_plane0, plane1[:, 0:N])
+        k["planes"] = (k_plane0, plane1[:, N : 2 * N])
         c_got = sb.tile([P, N], U32, align_bytes=64)
         nc.vector.tensor_copy(c_got[:], c["wwin"][:].bitcast(U32).indirect(c["offsets"][:]))
-        nc.vector.tensor_copy(planes[0][0:4, :].bitcast(I32), got_scales[0:4, :].bitcast(I32))
+        copy_rows(k_plane0, slice(N, 2 * N))
         quantise_pass(0)
         warm = ps.tile([P, N], F32)
         nc.tensor.matmul_mx(
@@ -131,9 +147,13 @@ def tile_attend_sumw_topk_kernel(tc, qT, k_words, k_scales, c_words, c_scales, o
             start=True,
             stop=True,
         )
-        c_parted = placed.tile([P, PASSES, 2 * N], U8, offset=512, align_bytes=64)
-        part_words(c_parted[:], c_got[:])
-        score_pass(c, 0, slice(0, N), c_parted[:, 0, :], True)
+        c_parted = [placed.tile([P, 2 * N], U8, name="c_parted%d" % o, offset=2304 + 1024 * o, align_bytes=64) for o in range(PASSES)]
+        for o in range(PASSES):
+            nc.vector.tensor_copy(
+                c_parted[o][:].bitcast(U16).rearrange("p (h n) -> p h n", h=2),
+                c_got[:].bitcast(U16).rearrange("p (h n o) -> p o h n", h=2, o=2)[:, o],
+            )
+        score_pass(c, 0, slice(0, N), c_parted[0][:], True)
         half = N // 2
         k_got = sb.tile([P, N], U32, tag="q_bf0", align_bytes=64)
         for h in range(2):
@@ -145,7 +165,7 @@ def tile_attend_sumw_topk_kernel(tc, qT, k_words, k_scales, c_words, c_scales, o
             part_words(pair[:], k_got[:, g * GROUP : (g + 1) * GROUP])
             if g == 0:
                 quantise_pass(1)
-                score_pass(c, 1, slice(0, N), c_parted[:, 1, :], False)
+                score_pass(c, 1, slice(0, N), c_parted[1][:], False)
             for o in (1, 0):
                 score_pass(k, o, slice(g * GROUP, (g + 1) * GROUP), pair[:, o, :], o == 1)
         softmax_terms(c, "k_wwin")

@@ -60,8 +60,8 @@ def tile_attend_sumw_topk_kernel(tc, qT, k_words, k_scales, c_words, c_scales, o
             rows = qT[0].rearrange("(o p t) m -> o p (t m)", o=PASSES, t=4)[o]
             nc.sync.dma_start(q_raw[o][:].rearrange("p t m -> p (t m)"), rows)
 
-        def load_words(t):
-            nc.sync.dma_start(t["wwin"][:], t["words"][0].rearrange("p t b -> p (t b)").bitcast(I32))
+        def load_words(t, cols):
+            nc.sync.dma_start(t["wwin"][:, cols], t["words"][0].rearrange("p t b -> p (t b)").bitcast(I32)[:, cols])
 
         for t in (c, k):
             for lo, hi in ((32, 64), (64, 128)):
@@ -70,9 +70,9 @@ def tile_attend_sumw_topk_kernel(tc, qT, k_words, k_scales, c_words, c_scales, o
             nc.sync.dma_start(t["offsets"][:], t["lst"])
             rows = t["scales"].rearrange("o f t -> (o f) t")
             nc.scalar.dma_start(t["swin"][0:ROWS, :].bitcast(I32), rows.bitcast(I32))
-        load_words(c)
+        load_words(c, slice(0, 1024))
         load_queries(0)
-        load_words(k)
+        load_words(k, slice(0, 1536))
 
         def gather_scales(t):
             nc.vector.tensor_copy(got_scales[:, t["first"] : t["first"] + N], t["swin"][:].indirect(t["offsets"][:]))
@@ -124,6 +124,7 @@ def tile_attend_sumw_topk_kernel(tc, qT, k_words, k_scales, c_words, c_scales, o
         gather_scales(c)
         c_plane0 = sb.tile([P, N], U8, align_bytes=64)
         move_rows(c_plane0, 0, range(4), slice(0, N))
+        load_words(k, slice(1536, 2048))
         load_queries(1)
         gather_scales(k)
         plane1 = sb.tile([P, 2 * N], U8, align_bytes=64)
@@ -135,8 +136,8 @@ def tile_attend_sumw_topk_kernel(tc, qT, k_words, k_scales, c_words, c_scales, o
         k["planes"] = (k_plane0, plane1[:, N : 2 * N])
         c_got = sb.tile([P, N], U32, align_bytes=64)
         nc.vector.tensor_copy(c_got[:], c["wwin"][:].bitcast(U32).indirect(c["offsets"][:]))
-        copy_rows(k_plane0, slice(N, 2 * N))
         quantise_pass(0)
+        copy_rows(k_plane0, slice(N, 2 * N))
         warm = ps.tile([P, N], F32)
         nc.tensor.matmul_mx(
             out=warm[:],
@@ -160,17 +161,16 @@ def tile_attend_sumw_topk_kernel(tc, qT, k_words, k_scales, c_words, c_scales, o
             lst = k["offsets"][:, h * half // 16 : (h + 1) * half // 16]
             nc.vector.tensor_copy(k_got[:, h * half : (h + 1) * half], k["wwin"][:].bitcast(U32).indirect(lst))
         cast_pass(1)
+        quantise_pass(1)
+        score_pass(c, 1, slice(0, N), c_parted[1][:], False)
         for g in range(N // GROUP):
-            pair = placed.tile([P, PASSES, 2 * GROUP], U8, name="k_pair%d" % g, offset=6656 - 4 * GROUP * g, align_bytes=64)
+            pair = placed.tile([P, PASSES, 2 * GROUP], U8, name="k_pair%d" % g, offset=6144 - 4 * GROUP * g, align_bytes=64)
             part_words(pair[:], k_got[:, g * GROUP : (g + 1) * GROUP])
-            if g == 0:
-                quantise_pass(1)
-                score_pass(c, 1, slice(0, N), c_parted[1][:], False)
             for o in (1, 0):
                 score_pass(k, o, slice(g * GROUP, (g + 1) * GROUP), pair[:, o, :], o == 1)
         softmax_terms(c, "k_wwin")
         softmax_terms(k, "k_nmax")
-        invert(c, placed.tile([P, 1], F32, name="c_inv", offset=6656 - 4 * GROUP * 3, align_bytes=64))
+        invert(c, placed.tile([P, 1], F32, name="c_inv", offset=6144 - 4 * GROUP * 3, align_bytes=64))
         nc.vector.tensor_scalar(part[:], c["e"][:], c["inv"][:], None, ALU.mult)
         invert(k, sb.tile([P, 1], F32, name="k_inv", align_bytes=64))
         for h in range(2):

@@ -138,22 +138,22 @@ def tile_attend_sumw_topk_kernel(tc, qT, k_words, k_scales, c_words, c_scales, o
         nc.vector.tensor_copy(c_got[:], c["wwin"][:].bitcast(U32).indirect(c["offsets"][:]))
         quantise_pass(0)
         copy_rows(k_plane0, slice(N, 2 * N))
-        warm = ps.tile([P, N], F32)
-        nc.tensor.matmul_mx(
-            out=warm[:],
-            lhsT=q_codes[:, 0:NQ].bitcast(FP8X4),
-            lhsT_scale=q_scales[:, 0:NQ],
-            rhs=c_got[:, 0 : N // 2].bitcast(FP4X4),
-            rhs_scale=got_scales[:, 0:N],
-            start=True,
-            stop=True,
-        )
         c_parted = [placed.tile([P, 2 * N], U8, name="c_parted%d" % o, offset=2304 + 1024 * o, align_bytes=64) for o in range(PASSES)]
         for o in range(PASSES):
             nc.vector.tensor_copy(
                 c_parted[o][:].bitcast(U16).rearrange("p (h n) -> p h n", h=2),
                 c_got[:].bitcast(U16).rearrange("p (h n o) -> p o h n", h=2, o=2)[:, o],
             )
+        warm = ps.tile([P, N], F32)
+        nc.tensor.matmul_mx(
+            out=warm[:],
+            lhsT=q_codes[:, 0:NQ].bitcast(FP8X4),
+            lhsT_scale=q_scales[:, 0:NQ],
+            rhs=c_parted[0][:].bitcast(FP4X4),
+            rhs_scale=got_scales[:, 0:N],
+            start=True,
+            stop=True,
+        )
         score_pass(c, 0, slice(0, N), c_parted[0][:], True)
         half = N // 2
         k_got = sb.tile([P, N], U32, tag="q_bf0", align_bytes=64)

@@ -19,10 +19,15 @@ NQ = 128
 N = 512
 D = 1024
 PASSES = 2
-GROUP = 128
+GROUP = 256
 ROWS = 32
 
 FLOPS = 2 * 2 * NQ * N * D
+
+PLANE0 = 2048
+Q_RAW = 0
+Q_BF = 4096
+K_LAST_PAIR = 6144
 
 
 def tile_attend_sumw_topk_kernel(tc, qT, k_words, k_scales, c_words, c_scales, offs, offs2, out):
@@ -33,148 +38,129 @@ def tile_attend_sumw_topk_kernel(tc, qT, k_words, k_scales, c_words, c_scales, o
         ps = ctx.enter_context(tc.psum_pool(name="ps", bufs=1))
 
         tables = {}
-        for name, words, scales, lst, first, at in (("c", c_words, c_scales, offs2, 0, 4608), ("k", k_words, k_scales, offs, N, 7168)):
+        for name, words, scales, lst, first in (("c", c_words, c_scales, offs2, 0), ("k", k_words, k_scales, offs, N)):
             t = words.shape[2]
             tables[name] = dict(
-                words=words,
-                scales=scales,
+                words=words[0].rearrange("p t b -> p (t b)").bitcast(I32),
+                scales=scales.rearrange("o f t -> (o f) t").bitcast(I32),
                 lst=lst,
                 offsets=sb.tile([P, N // 16], U16, name=name + "_offsets"),
-                wwin=sb.tile([P, t], I32, name=name + "_wwin", tag=name + "_wwin", align_bytes=64),
-                swin=placed.tile([P, t], U8, name=name + "_swin", offset=at, align_bytes=64),
-                first=first,
+                wwin=sb.tile([P, t], I32, name=name + "_wwin", align_bytes=64),
+                swin=sb.tile([P, t], U8, name=name + "_swin", align_bytes=64),
+                cols=slice(first, first + N),
                 acc=ps.tile([P, N], F32, name=name + "_acc"),
                 e=sb.tile([P, N], F32, name=name + "_e", align_bytes=64),
                 total=sb.tile([P, 1], F32, name=name + "_total"),
             )
         c, k = tables["c"], tables["k"]
-        q_raw = {}
-        q_bf = [sb.tile([P, NQ, 4], BF16, name="q_bf%d" % o, tag="q_bf%d" % o, align_bytes=64) for o in range(PASSES)]
+        q_raw = placed.tile([P, PASSES, 4 * NQ], F32, offset=Q_RAW, align_bytes=64)
+        q_bf = placed.tile([P, PASSES, 4 * NQ], BF16, offset=Q_BF, align_bytes=64)
         q_codes = sb.tile([P, PASSES * NQ], U32, align_bytes=64)
         q_scales = sb.tile([P, PASSES * NQ], U8, align_bytes=64)
         got_scales = sb.tile([P, 2 * N], U8, align_bytes=64)
         part = sb.tile([P, N], F32, align_bytes=64)
 
-        def load_queries(o):
-            q_raw[o] = placed.tile([P, 4, NQ], F32, name="q_raw%d" % o, offset=(2048, 4608)[o], align_bytes=64)
-            rows = qT[0].rearrange("(o p t) m -> o p (t m)", o=PASSES, t=4)[o]
-            nc.sync.dma_start(q_raw[o][:].rearrange("p t m -> p (t m)"), rows)
-
-        def load_words(t, cols):
-            nc.sync.dma_start(t["wwin"][:, cols], t["words"][0].rearrange("p t b -> p (t b)").bitcast(I32)[:, cols])
-
         for t in (c, k):
             for lo, hi in ((32, 64), (64, 128)):
                 nc.vector.memset(t["swin"][lo:hi, :].bitcast(I32), 0)
         for t in (c, k):
-            nc.sync.dma_start(t["offsets"][:], t["lst"])
-            rows = t["scales"].rearrange("o f t -> (o f) t")
-            nc.scalar.dma_start(t["swin"][0:ROWS, :].bitcast(I32), rows.bitcast(I32))
-        load_words(c, slice(0, 1024))
-        load_queries(0)
-        load_words(k, slice(0, 1536))
+            nc.scalar.dma_start(t["swin"][0:ROWS, :].bitcast(I32), t["scales"])
+        nc.sync.dma_start(c["offsets"][:], c["lst"])
+        nc.sync.dma_start(k["offsets"][:], k["lst"])
+        nc.sync.dma_start(c["wwin"][:], c["words"])
+        nc.scalar.dma_start(q_raw[:], qT[0].rearrange("(o p t) m -> p o (t m)", o=PASSES, t=4))
+        nc.scalar.dma_start(k["wwin"][:], k["words"])
 
         def gather_scales(t):
-            nc.vector.tensor_copy(got_scales[:, t["first"] : t["first"] + N], t["swin"][:].indirect(t["offsets"][:]))
+            nc.vector.tensor_copy(got_scales[:, t["cols"]], t["swin"][:].indirect(t["offsets"][:]))
 
-        def score_pass(t, o, cols, words, first):
+        def move_rows(plane, o, quads):
+            for quad in quads:
+                at = 16 * o + 4 * quad
+                nc.sync.dma_start(plane[32 * quad : 32 * quad + 4, :].bitcast(I32), got_scales[at : at + 4, :].bitcast(I32))
+
+        def score_pass(t, o, cols, words, start, stop):
             nc.tensor.matmul_mx(
                 out=t["acc"][:, cols],
                 lhsT=q_codes[:, o * NQ : (o + 1) * NQ].bitcast(FP8X4),
                 lhsT_scale=q_scales[:, o * NQ : (o + 1) * NQ],
                 rhs=words.bitcast(FP4X4),
                 rhs_scale=t["planes"][o][:, cols],
-                start=first,
-                stop=not first,
+                start=start,
+                stop=stop,
             )
-
-        def softmax_terms(t, slot):
-            t["nmax"] = sb.tile([P, 1], F32, name=slot + "_nmax", tag=slot, align_bytes=64)
-            nc.vector.tensor_reduce(t["nmax"][:], t["acc"][:], AX.X, ALU.max, negate=True)
-            nc.scalar.activation(t["e"][:], t["acc"][:], ACT.Exp, bias=t["nmax"][:], accum_out=t["total"][:])
-
-        def invert(t, inv):
-            t["inv"] = inv
-            nc.vector.reciprocal(t["inv"][:], t["total"][:])
 
         def cast_pass(o):
             nc.scalar.copy(
-                q_bf[o][:].rearrange("p (m i) t -> p m t i", i=4),
-                q_raw[o][:].rearrange("p t (m i) -> p m t i", i=4),
+                q_bf[:, o, :].rearrange("p (m i t) -> p m t i", i=4, t=4),
+                q_raw[:, o, :].rearrange("p (t m i) -> p m t i", t=4, i=4),
             )
 
-        def quantise_pass(o):
-            nc.vector.quantize_mx(
-                out=q_codes[:, o * NQ : (o + 1) * NQ].bitcast(FP8X4),
-                scales=q_scales[:, o * NQ : (o + 1) * NQ],
-                in_=q_bf[o][:].rearrange("p m t -> p (m t)"),
-            )
+        def part_words(pair, got):
+            nc.vector.tensor_copy(pair[:].bitcast(U16), got[:].bitcast(U16).rearrange("p (n o) -> p o n", o=2))
 
-        def part_words(parted, words):
-            nc.vector.tensor_copy(parted.bitcast(U16), words.bitcast(U16).rearrange("p (n o) -> p o n", o=2))
-
-        def move_rows(plane, o, quads, cols):
-            for quad in quads:
-                at = 16 * o + 4 * quad
-                nc.sync.dma_start(plane[32 * quad : 32 * quad + 4, :].bitcast(I32), got_scales[at : at + 4, cols].bitcast(I32))
-
-        def copy_rows(plane, cols):
-            nc.vector.tensor_copy(plane[0:4, :].bitcast(I32), got_scales[0:4, cols].bitcast(I32))
+        def softmax_terms(t, nmax):
+            nc.vector.tensor_reduce(nmax[:], t["acc"][:], AX.X, ALU.max, negate=True)
+            nc.scalar.activation(t["e"][:], t["acc"][:], ACT.Exp, bias=nmax[:], accum_out=t["total"][:])
 
         gather_scales(c)
-        c_plane0 = sb.tile([P, N], U8, align_bytes=64)
-        move_rows(c_plane0, 0, range(4), slice(0, N))
-        load_words(k, slice(1536, 2048))
-        load_queries(1)
         gather_scales(k)
         plane1 = sb.tile([P, 2 * N], U8, align_bytes=64)
-        move_rows(plane1, 1, range(4), slice(0, 2 * N))
-        cast_pass(0)
-        k_plane0 = placed.tile([P, N], U8, offset=1792, align_bytes=64)
-        move_rows(k_plane0, 0, (1, 2, 3), slice(N, 2 * N))
-        c["planes"] = (c_plane0, plane1[:, 0:N])
-        k["planes"] = (k_plane0, plane1[:, N : 2 * N])
+        move_rows(plane1, 1, range(4))
+        for o in range(PASSES):
+            cast_pass(o)
+        plane0 = placed.tile([P, 2 * N], U8, offset=PLANE0, align_bytes=64)
+        move_rows(plane0, 0, range(1, 4))
+        for t in (c, k):
+            t["planes"] = (plane0[:, t["cols"]], plane1[:, t["cols"]])
+
         c_got = sb.tile([P, N], U32, align_bytes=64)
         nc.vector.tensor_copy(c_got[:], c["wwin"][:].bitcast(U32).indirect(c["offsets"][:]))
-        quantise_pass(0)
-        copy_rows(k_plane0, slice(N, 2 * N))
-        c_parted = [placed.tile([P, 2 * N], U8, name="c_parted%d" % o, offset=2304 + 1024 * o, align_bytes=64) for o in range(PASSES)]
-        for o in range(PASSES):
-            nc.vector.tensor_copy(
-                c_parted[o][:].bitcast(U16).rearrange("p (h n) -> p h n", h=2),
-                c_got[:].bitcast(U16).rearrange("p (h n o) -> p o h n", h=2, o=2)[:, o],
-            )
-        warm = ps.tile([P, N], F32)
+        nc.vector.quantize_mx(out=q_codes[:].bitcast(FP8X4), scales=q_scales[:], in_=q_bf[:].rearrange("p o x -> p (o x)"))
+        c_pair = placed.tile([P, PASSES, 2 * N], U8, offset=Q_RAW, align_bytes=64)
+        part_words(c_pair, c_got)
+        nc.vector.tensor_copy(plane0[0:4, :].bitcast(I32), got_scales[0:4, :].bitcast(I32))
+        warm = ps.tile([P, NQ], F32)
         nc.tensor.matmul_mx(
             out=warm[:],
-            lhsT=q_codes[:, 0:NQ].bitcast(FP8X4),
-            lhsT_scale=q_scales[:, 0:NQ],
-            rhs=c_parted[0][:].bitcast(FP4X4),
-            rhs_scale=got_scales[:, 0:N],
+            lhsT=q_codes[:, NQ : 2 * NQ].bitcast(FP8X4),
+            lhsT_scale=q_scales[:, NQ : 2 * NQ],
+            rhs=c_pair[:, 1, 0 : 2 * NQ].bitcast(FP4X4),
+            rhs_scale=plane1[:, 0:NQ],
             start=True,
             stop=True,
         )
-        score_pass(c, 0, slice(0, N), c_parted[0][:], True)
-        half = N // 2
-        k_got = sb.tile([P, N], U32, tag="q_bf0", align_bytes=64)
-        for h in range(2):
-            lst = k["offsets"][:, h * half // 16 : (h + 1) * half // 16]
-            nc.vector.tensor_copy(k_got[:, h * half : (h + 1) * half], k["wwin"][:].bitcast(U32).indirect(lst))
-        cast_pass(1)
-        quantise_pass(1)
-        score_pass(c, 1, slice(0, N), c_parted[1][:], False)
+        score_pass(c, 1, slice(0, N), c_pair[:, 1, :], True, False)
+        for lo, hi in ((0, 256), (256, 384), (384, N)):
+            score_pass(c, 0, slice(lo, hi), c_pair[:, 0, 2 * lo : 2 * hi], False, hi == N)
+
+        k_got = {}
+
+        def gather_group(g):
+            k_got[g] = placed.tile([P, GROUP], U32, name="k_got%d" % g, offset=Q_BF + 4 * GROUP * g, align_bytes=64)
+            lst = k["offsets"][:, g * GROUP // 16 : (g + 1) * GROUP // 16]
+            nc.vector.tensor_copy(k_got[g][:], k["wwin"][:].bitcast(U32).indirect(lst))
+
+        def score_group(g):
+            pair = placed.tile([P, PASSES, 2 * GROUP], U8, name="k_pair%d" % g, offset=K_LAST_PAIR + 4 * GROUP * (1 - g), align_bytes=64)
+            part_words(pair, k_got[g])
+            for o in range(PASSES):
+                score_pass(k, o, slice(g * GROUP, (g + 1) * GROUP), pair[:, o, :], o == 0, o == 1)
+
         for g in range(N // GROUP):
-            pair = placed.tile([P, PASSES, 2 * GROUP], U8, name="k_pair%d" % g, offset=6144 - 4 * GROUP * g, align_bytes=64)
-            part_words(pair[:], k_got[:, g * GROUP : (g + 1) * GROUP])
-            for o in (1, 0):
-                score_pass(k, o, slice(g * GROUP, (g + 1) * GROUP), pair[:, o, :], o == 1)
-        softmax_terms(c, "k_wwin")
-        softmax_terms(k, "k_nmax")
-        invert(c, placed.tile([P, 1], F32, name="c_inv", offset=6144 - 4 * GROUP * 3, align_bytes=64))
-        nc.vector.tensor_scalar(part[:], c["e"][:], c["inv"][:], None, ALU.mult)
-        invert(k, sb.tile([P, 1], F32, name="k_inv", align_bytes=64))
+            gather_group(g)
+        for g in range(N // GROUP):
+            score_group(g)
+
+        softmax_terms(c, placed.tile([P, 1], F32, name="c_nmax", offset=Q_BF, align_bytes=64))
+        softmax_terms(k, sb.tile([P, 1], F32, name="k_nmax", align_bytes=64))
+        c_inv = placed.tile([P, 1], F32, offset=K_LAST_PAIR, align_bytes=64)
+        nc.vector.reciprocal(c_inv[:], c["total"][:])
+        nc.vector.tensor_scalar(part[:], c["e"][:], c_inv[:], None, ALU.mult)
+        k_inv = sb.tile([P, 1], F32, align_bytes=64)
+        nc.vector.reciprocal(k_inv[:], k["total"][:])
         for h in range(2):
             cols = slice(h * N // 2, (h + 1) * N // 2)
             res = sb.tile([P, N // 2], F32, name="res%d" % h, align_bytes=64)
-            nc.vector.scalar_tensor_tensor(res[:], k["e"][:, cols], k["inv"][:], part[:, cols], ALU.mult, ALU.add)
+            nc.vector.scalar_tensor_tensor(res[:], k["e"][:, cols], k_inv[:], part[:, cols], ALU.mult, ALU.add)
             nc.sync.dma_start(out[0][:, cols], res[:])

@@ -97,7 +97,7 @@ def tile_attend_sumw_topk_kernel(tc, qT, k_words, k_scales, c_words, c_scales, o
             )
 
         def part_words(pair, got):
-            nc.vector.tensor_copy(pair[:].bitcast(U16), got[:].bitcast(U16).rearrange("p (n o) -> p o n", o=2))
+            nc.vector.tensor_copy(pair[:].bitcast(U16), got.bitcast(U16).rearrange("p (n o) -> p o n", o=2))
 
         def softmax_terms(t, nmax):
             nc.vector.tensor_reduce(nmax[:], t["acc"][:], AX.X, ALU.max, negate=True)
@@ -117,22 +117,27 @@ def tile_attend_sumw_topk_kernel(tc, qT, k_words, k_scales, c_words, c_scales, o
         c_got = sb.tile([P, N], U32, align_bytes=64)
         nc.vector.tensor_copy(c_got[:], c["wwin"][:].bitcast(U32).indirect(c["offsets"][:]))
         nc.vector.quantize_mx(out=q_codes[:].bitcast(FP8X4), scales=q_scales[:], in_=q_bf[:].rearrange("p o x -> p (o x)"))
-        c_pair = placed.tile([P, PASSES, 2 * N], U8, offset=Q_RAW, align_bytes=64)
-        part_words(c_pair, c_got)
+        c_parted = {}
+        for o in (1, 0):
+            c_parted[o] = placed.tile([P, 2 * N], U8, name="c_parted%d" % o, offset=Q_RAW + 2 * N * o, align_bytes=64)
+            nc.vector.tensor_copy(
+                c_parted[o][:].bitcast(U16).rearrange("p (h n) -> p h n", h=2),
+                c_got[:].bitcast(U16).rearrange("p (h n o) -> p o h n", h=2, o=2)[:, o],
+            )
         nc.vector.tensor_copy(plane0[0:4, :].bitcast(I32), got_scales[0:4, :].bitcast(I32))
         warm = ps.tile([P, NQ], F32)
         nc.tensor.matmul_mx(
             out=warm[:],
             lhsT=q_codes[:, NQ : 2 * NQ].bitcast(FP8X4),
             lhsT_scale=q_scales[:, NQ : 2 * NQ],
-            rhs=c_pair[:, 1, 0 : 2 * NQ].bitcast(FP4X4),
+            rhs=c_parted[1][:, 0 : 2 * NQ].bitcast(FP4X4),
             rhs_scale=plane1[:, 0:NQ],
             start=True,
             stop=True,
         )
-        score_pass(c, 1, slice(0, N), c_pair[:, 1, :], True, False)
+        score_pass(c, 1, slice(0, N), c_parted[1][:], True, False)
         for lo, hi in ((0, 256), (256, 384), (384, N)):
-            score_pass(c, 0, slice(lo, hi), c_pair[:, 0, 2 * lo : 2 * hi], False, hi == N)
+            score_pass(c, 0, slice(lo, hi), c_parted[0][:, 2 * lo : 2 * hi], False, hi == N)
 
         k_got = {}
 
@@ -141,16 +146,16 @@ def tile_attend_sumw_topk_kernel(tc, qT, k_words, k_scales, c_words, c_scales, o
             lst = k["offsets"][:, g * GROUP // 16 : (g + 1) * GROUP // 16]
             nc.vector.tensor_copy(k_got[g][:], k["wwin"][:].bitcast(U32).indirect(lst))
 
-        def score_group(g):
-            pair = placed.tile([P, PASSES, 2 * GROUP], U8, name="k_pair%d" % g, offset=K_LAST_PAIR + 4 * GROUP * (1 - g), align_bytes=64)
-            part_words(pair, k_got[g])
+        def score_group(lo, hi):
+            pair = placed.tile([P, PASSES, 2 * (hi - lo)], U8, name="k_pair%d" % lo, offset=K_LAST_PAIR + 4 * (N - hi), align_bytes=64)
+            part_words(pair, k_got[lo // GROUP][:, lo % GROUP : lo % GROUP + hi - lo])
             for o in range(PASSES):
-                score_pass(k, o, slice(g * GROUP, (g + 1) * GROUP), pair[:, o, :], o == 0, o == 1)
+                score_pass(k, o, slice(lo, hi), pair[:, o, :], o == 0, o == 1)
 
         for g in range(N // GROUP):
             gather_group(g)
-        for g in range(N // GROUP):
-            score_group(g)
+        for lo, hi in ((0, 128), (128, 256), (256, 384), (384, N)):
+            score_group(lo, hi)
 
         softmax_terms(c, placed.tile([P, 1], F32, name="c_nmax", offset=Q_BF, align_bytes=64))
         softmax_terms(k, sb.tile([P, 1], F32, name="k_nmax", align_bytes=64))

@@ -24,8 +24,8 @@ ROWS = 32
 
 FLOPS = 2 * 2 * NQ * N * D
 
-PLANE0 = 2048
 Q_RAW = 0
+PLANES = (2048, 3072)
 Q_BF = 4096
 K_LAST_PAIR = 6144
 
@@ -67,17 +67,17 @@ def tile_attend_sumw_topk_kernel(tc, qT, k_words, k_scales, c_words, c_scales, o
             nc.scalar.dma_start(t["swin"][0:ROWS, :].bitcast(I32), t["scales"])
         nc.sync.dma_start(c["offsets"][:], c["lst"])
         nc.sync.dma_start(k["offsets"][:], k["lst"])
-        nc.sync.dma_start(c["wwin"][:], c["words"])
         nc.scalar.dma_start(q_raw[:], qT[0].rearrange("(o p t) m -> p o (t m)", o=PASSES, t=4))
+        nc.scalar.dma_start(c["wwin"][:], c["words"])
         nc.scalar.dma_start(k["wwin"][:], k["words"])
 
         def gather_scales(t):
             nc.vector.tensor_copy(got_scales[:, t["cols"]], t["swin"][:].indirect(t["offsets"][:]))
 
-        def move_rows(plane, o, quads):
+        def move_rows(plane, o, quads, cols):
             for quad in quads:
                 at = 16 * o + 4 * quad
-                nc.sync.dma_start(plane[32 * quad : 32 * quad + 4, :].bitcast(I32), got_scales[at : at + 4, :].bitcast(I32))
+                nc.sync.dma_start(plane[32 * quad : 32 * quad + 4, cols].bitcast(I32), got_scales[at : at + 4, cols].bitcast(I32))
 
         def score_pass(t, o, cols, words, start, stop):
             nc.tensor.matmul_mx(
@@ -105,39 +105,40 @@ def tile_attend_sumw_topk_kernel(tc, qT, k_words, k_scales, c_words, c_scales, o
 
         gather_scales(c)
         gather_scales(k)
-        plane1 = sb.tile([P, 2 * N], U8, align_bytes=64)
-        move_rows(plane1, 1, range(4))
+        both = slice(0, 2 * N)
         for o in range(PASSES):
             cast_pass(o)
-        plane0 = placed.tile([P, 2 * N], U8, offset=PLANE0, align_bytes=64)
-        move_rows(plane0, 0, range(1, 4))
+        plane0 = placed.tile([P, 2 * N], U8, offset=PLANES[0], align_bytes=64)
+        move_rows(plane0, 0, range(1, 4), both)
+        plane1 = placed.tile([P, 2 * N], U8, offset=PLANES[1], align_bytes=64)
+        move_rows(plane1, 1, range(4), both)
         for t in (c, k):
             t["planes"] = (plane0[:, t["cols"]], plane1[:, t["cols"]])
 
         c_got = sb.tile([P, N], U32, align_bytes=64)
         nc.vector.tensor_copy(c_got[:], c["wwin"][:].bitcast(U32).indirect(c["offsets"][:]))
         nc.vector.quantize_mx(out=q_codes[:].bitcast(FP8X4), scales=q_scales[:], in_=q_bf[:].rearrange("p o x -> p (o x)"))
+        nc.vector.tensor_copy(plane0[0:4, :].bitcast(I32), got_scales[0:4, :].bitcast(I32))
         c_parted = {}
-        for o in (1, 0):
+        for o in range(PASSES):
             c_parted[o] = placed.tile([P, 2 * N], U8, name="c_parted%d" % o, offset=Q_RAW + 2 * N * o, align_bytes=64)
             nc.vector.tensor_copy(
                 c_parted[o][:].bitcast(U16).rearrange("p (h n) -> p h n", h=2),
                 c_got[:].bitcast(U16).rearrange("p (h n o) -> p o h n", h=2, o=2)[:, o],
             )
-        nc.vector.tensor_copy(plane0[0:4, :].bitcast(I32), got_scales[0:4, :].bitcast(I32))
         warm = ps.tile([P, NQ], F32)
         nc.tensor.matmul_mx(
             out=warm[:],
-            lhsT=q_codes[:, NQ : 2 * NQ].bitcast(FP8X4),
-            lhsT_scale=q_scales[:, NQ : 2 * NQ],
-            rhs=c_parted[1][:, 0 : 2 * NQ].bitcast(FP4X4),
-            rhs_scale=plane1[:, 0:NQ],
+            lhsT=q_codes[:, 0:NQ].bitcast(FP8X4),
+            lhsT_scale=q_scales[:, 0:NQ],
+            rhs=c_parted[0][:, 0 : 2 * NQ].bitcast(FP4X4),
+            rhs_scale=got_scales[:, 0:NQ],
             start=True,
             stop=True,
         )
-        score_pass(c, 1, slice(0, N), c_parted[1][:], True, False)
+        score_pass(c, 0, slice(0, N), c_parted[0][:], True, False)
         for lo, hi in ((0, 256), (256, 384), (384, N)):
-            score_pass(c, 0, slice(lo, hi), c_parted[0][:, 2 * lo : 2 * hi], False, hi == N)
+            score_pass(c, 1, slice(lo, hi), c_parted[1][:, 2 * lo : 2 * hi], False, hi == N)
 
         k_got = {}
 
@@ -149,8 +150,8 @@ def tile_attend_sumw_topk_kernel(tc, qT, k_words, k_scales, c_words, c_scales, o
         def score_group(lo, hi):
             pair = placed.tile([P, PASSES, 2 * (hi - lo)], U8, name="k_pair%d" % lo, offset=K_LAST_PAIR + 4 * (N - hi), align_bytes=64)
             part_words(pair, k_got[lo // GROUP][:, lo % GROUP : lo % GROUP + hi - lo])
-            for o in range(PASSES):
-                score_pass(k, o, slice(lo, hi), pair[:, o, :], o == 0, o == 1)
+            for o in (1, 0):
+                score_pass(k, o, slice(lo, hi), pair[:, o, :], o == 1, o == 0)
 
         for g in range(N // GROUP):
             gather_group(g)

@@ -126,16 +126,6 @@ def tile_attend_sumw_topk_kernel(tc, qT, k_words, k_scales, c_words, c_scales, o
                 c_parted[o][:].bitcast(U16).rearrange("p (h n) -> p h n", h=2),
                 c_got[:].bitcast(U16).rearrange("p (h n o) -> p o h n", h=2, o=2)[:, o],
             )
-        warm = ps.tile([P, NQ], F32)
-        nc.tensor.matmul_mx(
-            out=warm[:],
-            lhsT=q_codes[:, 0:NQ].bitcast(FP8X4),
-            lhsT_scale=q_scales[:, 0:NQ],
-            rhs=c_parted[0][:, 0 : 2 * NQ].bitcast(FP4X4),
-            rhs_scale=got_scales[:, 0:NQ],
-            start=True,
-            stop=True,
-        )
         score_pass(c, 0, slice(0, N), c_parted[0][:], True, False)
         for lo, hi in ((0, 256), (256, 384), (384, N)):
             score_pass(c, 1, slice(lo, hi), c_parted[1][:, 2 * lo : 2 * hi], False, hi == N)

@@ -19,7 +19,7 @@ NQ = 128
 N = 512
 D = 1024
 PASSES = 2
-GROUP = 256
+K_FIRST = 384
 ROWS = 32
 
 FLOPS = 2 * 2 * NQ * N * D
@@ -126,29 +126,27 @@ def tile_attend_sumw_topk_kernel(tc, qT, k_words, k_scales, c_words, c_scales, o
                 c_parted[o][:].bitcast(U16).rearrange("p (h n) -> p h n", h=2),
                 c_got[:].bitcast(U16).rearrange("p (h n o) -> p o h n", h=2, o=2)[:, o],
             )
-        score_pass(c, 0, slice(0, N), c_parted[0][:], True, False)
-        for lo, hi in ((0, 256), (256, 384), (384, N)):
-            score_pass(c, 1, slice(lo, hi), c_parted[1][:, 2 * lo : 2 * hi], False, hi == N)
+        for o in range(PASSES):
+            score_pass(c, o, slice(0, N), c_parted[o][:], o == 0, o == 1)
 
-        k_got = {}
+        def gather_k(lo, hi):
+            got = placed.tile([P, hi - lo], U32, name="k_got%d" % lo, offset=Q_BF + 4 * lo, align_bytes=64)
+            nc.vector.tensor_copy(got[:], k["wwin"][:].bitcast(U32).indirect(k["offsets"][:, lo // 16 : hi // 16]))
+            return got
 
-        def gather_group(g):
-            k_got[g] = placed.tile([P, GROUP], U32, name="k_got%d" % g, offset=Q_BF + 4 * GROUP * g, align_bytes=64)
-            lst = k["offsets"][:, g * GROUP // 16 : (g + 1) * GROUP // 16]
-            nc.vector.tensor_copy(k_got[g][:], k["wwin"][:].bitcast(U32).indirect(lst))
-
-        def score_group(lo, hi):
+        def score_group(lo, hi, got):
             pair = placed.tile([P, PASSES, 2 * (hi - lo)], U8, name="k_pair%d" % lo, offset=K_LAST_PAIR + 4 * (N - hi), align_bytes=64)
-            part_words(pair, k_got[lo // GROUP][:, lo % GROUP : lo % GROUP + hi - lo])
+            part_words(pair, got)
             for o in (1, 0):
                 score_pass(k, o, slice(lo, hi), pair[:, o, :], o == 1, o == 0)
 
-        for g in range(N // GROUP):
-            gather_group(g)
-        for lo, hi in ((0, 128), (128, 256), (256, 384), (384, N)):
-            score_group(lo, hi)
+        first = gather_k(0, K_FIRST)
+        last = gather_k(K_FIRST, N)
+        score_group(0, 128, first[:, 0:128])
+        score_group(128, K_FIRST, first[:, 128:K_FIRST])
+        score_group(K_FIRST, N, last[:])
 
-        softmax_terms(c, placed.tile([P, 1], F32, name="c_nmax", offset=Q_BF, align_bytes=64))
+        softmax_terms(c, sb.tile([P, 1], F32, name="c_nmax", align_bytes=64))
         softmax_terms(k, sb.tile([P, 1], F32, name="k_nmax", align_bytes=64))
         c_inv = placed.tile([P, 1], F32, offset=K_LAST_PAIR, align_bytes=64)
         nc.vector.reciprocal(c_inv[:], c["total"][:])

@@ -126,8 +126,9 @@ def tile_attend_sumw_topk_kernel(tc, qT, k_words, k_scales, c_words, c_scales, o
                 c_parted[o][:].bitcast(U16).rearrange("p (h n) -> p h n", h=2),
                 c_got[:].bitcast(U16).rearrange("p (h n o) -> p o h n", h=2, o=2)[:, o],
             )
-        for o in range(PASSES):
-            score_pass(c, o, slice(0, N), c_parted[o][:], o == 0, o == 1)
+        score_pass(c, 0, slice(0, N), c_parted[0][:], True, False)
+        for lo, hi in ((0, 256), (256, 384), (384, N)):
+            score_pass(c, 1, slice(lo, hi), c_parted[1][:, 2 * lo : 2 * hi], False, hi == N)
 
         def gather_k(lo, hi):
             got = placed.tile([P, hi - lo], U32, name="k_got%d" % lo, offset=Q_BF + 4 * lo, align_bytes=64)

@@ -25,7 +25,6 @@ ROWS = 32
 FLOPS = 2 * 2 * NQ * N * D
 
 Q_RAW = 0
-PLANES = (2048, 3072)
 Q_BF = 4096
 K_LAST_PAIR = 6144
 
@@ -42,7 +41,7 @@ def tile_attend_sumw_topk_kernel(tc, qT, k_words, k_scales, c_words, c_scales, o
             t = words.shape[2]
             tables[name] = dict(
                 words=words[0].rearrange("p t b -> p (t b)").bitcast(I32),
-                scales=scales.rearrange("o f t -> (o f) t").bitcast(I32),
+                scales=scales.bitcast(I32).rearrange("o f t -> f o t"),
                 lst=lst,
                 offsets=sb.tile([P, N // 16], U16, name=name + "_offsets"),
                 wwin=sb.tile([P, t], I32, name=name + "_wwin", align_bytes=64),
@@ -74,10 +73,8 @@ def tile_attend_sumw_topk_kernel(tc, qT, k_words, k_scales, c_words, c_scales, o
         def gather_scales(t):
             nc.vector.tensor_copy(got_scales[:, t["cols"]], t["swin"][:].indirect(t["offsets"][:]))
 
-        def move_rows(plane, o, quads, cols):
-            for quad in quads:
-                at = 16 * o + 4 * quad
-                nc.sync.dma_start(plane[32 * quad : 32 * quad + 4, cols].bitcast(I32), got_scales[at : at + 4, cols].bitcast(I32))
+        def move_rows(quad, cols):
+            nc.sync.dma_start(planes[32 * quad : 32 * quad + 4, :, cols].bitcast(I32), got_scales[8 * quad : 8 * quad + 8, cols].bitcast(I32))
 
         def score_pass(t, o, cols, words, start, stop):
             nc.tensor.matmul_mx(
@@ -103,22 +100,22 @@ def tile_attend_sumw_topk_kernel(tc, qT, k_words, k_scales, c_words, c_scales, o
             nc.vector.tensor_reduce(nmax[:], t["acc"][:], AX.X, ALU.max, negate=True)
             nc.scalar.activation(t["e"][:], t["acc"][:], ACT.Exp, bias=nmax[:], accum_out=t["total"][:])
 
+        planes = sb.tile([P, PASSES, 2 * N], U8, align_bytes=64)
         gather_scales(c)
+        for quad in range(3):
+            move_rows(quad, c["cols"])
         gather_scales(k)
-        both = slice(0, 2 * N)
+        move_rows(3, slice(0, 2 * N))
+        for quad in range(3):
+            move_rows(quad, k["cols"])
         for o in range(PASSES):
             cast_pass(o)
-        plane0 = placed.tile([P, 2 * N], U8, offset=PLANES[0], align_bytes=64)
-        move_rows(plane0, 0, range(1, 4), both)
-        plane1 = placed.tile([P, 2 * N], U8, offset=PLANES[1], align_bytes=64)
-        move_rows(plane1, 1, range(4), both)
         for t in (c, k):
-            t["planes"] = (plane0[:, t["cols"]], plane1[:, t["cols"]])
+            t["planes"] = [planes[:, o, t["cols"]] for o in range(PASSES)]
 
         c_got = sb.tile([P, N], U32, align_bytes=64)
         nc.vector.tensor_copy(c_got[:], c["wwin"][:].bitcast(U32).indirect(c["offsets"][:]))
         nc.vector.quantize_mx(out=q_codes[:].bitcast(FP8X4), scales=q_scales[:], in_=q_bf[:].rearrange("p o x -> p (o x)"))
-        nc.vector.tensor_copy(plane0[0:4, :].bitcast(I32), got_scales[0:4, :].bitcast(I32))
         c_parted = {}
         for o in range(PASSES):
             c_parted[o] = placed.tile([P, 2 * N], U8, name="c_parted%d" % o, offset=Q_RAW + 2 * N * o, align_bytes=64)

from contextlib import ExitStack

import concourse.mybir as mybir

F32 = mybir.dt.float32
BF16 = mybir.dt.bfloat16
I32 = mybir.dt.int32
U32 = mybir.dt.uint32
U16 = mybir.dt.uint16
U8 = mybir.dt.uint8
FP8X4 = mybir.dt.float8_e4m3fn_x4
FP4X4 = mybir.dt.float4_e2m1fn_x4
ALU = mybir.AluOpType
ACT = mybir.ActivationFunctionType
AX = mybir.AxisListType

P = 128
NQ = 128
N = 512
D = 1024
PASSES = 2
K_FIRST = 384
ROWS = 32

FLOPS = 2 * 2 * NQ * N * D

Q_RAW = 0
Q_BF = 4096
K_LAST_PAIR = 6144


def tile_attend_sumw_topk_kernel(tc, qT, k_words, k_scales, c_words, c_scales, offs, offs2, out):
    nc = tc.nc
    with ExitStack() as ctx:
        sb = ctx.enter_context(tc.tile_pool(name="sb", bufs=1))
        placed = ctx.enter_context(tc.tile_pool(name="placed", bufs=1))
        ps = ctx.enter_context(tc.psum_pool(name="ps", bufs=1))

        tables = {}
        for name, words, scales, lst, first in (("c", c_words, c_scales, offs2, 0), ("k", k_words, k_scales, offs, N)):
            t = words.shape[2]
            tables[name] = dict(
                words=words[0].rearrange("p t b -> p (t b)").bitcast(I32),
                scales=scales.bitcast(I32).rearrange("o f t -> f o t"),
                lst=lst,
                offsets=sb.tile([P, N // 16], U16, name=name + "_offsets"),
                wwin=sb.tile([P, t], I32, name=name + "_wwin", align_bytes=64),
                swin=sb.tile([P, t], U8, name=name + "_swin", align_bytes=64),
                cols=slice(first, first + N),
                acc=ps.tile([P, N], F32, name=name + "_acc"),
                e=sb.tile([P, N], F32, name=name + "_e", align_bytes=64),
                total=sb.tile([P, 1], F32, name=name + "_total"),
            )
        c, k = tables["c"], tables["k"]
        q_raw = placed.tile([P, PASSES, 4 * NQ], F32, offset=Q_RAW, align_bytes=64)
        q_bf = placed.tile([P, PASSES, 4 * NQ], BF16, offset=Q_BF, align_bytes=64)
        q_codes = sb.tile([P, PASSES * NQ], U32, align_bytes=64)
        q_scales = sb.tile([P, PASSES * NQ], U8, align_bytes=64)
        got_scales = sb.tile([P, 2 * N], U8, align_bytes=64)
        part = sb.tile([P, N], F32, align_bytes=64)

        for t in (c, k):
            for lo, hi in ((32, 64), (64, 128)):
                nc.vector.memset(t["swin"][lo:hi, :].bitcast(I32), 0)
        for t in (c, k):
            nc.scalar.dma_start(t["swin"][0:ROWS, :].bitcast(I32), t["scales"])
        nc.sync.dma_start(c["offsets"][:], c["lst"])
        nc.sync.dma_start(k["offsets"][:], k["lst"])
        nc.scalar.dma_start(q_raw[:], qT[0].rearrange("(o p t) m -> p o (t m)", o=PASSES, t=4))
        nc.scalar.dma_start(c["wwin"][:], c["words"])
        nc.scalar.dma_start(k["wwin"][:], k["words"])

        def gather_scales(t):
            nc.vector.tensor_copy(got_scales[:, t["cols"]], t["swin"][:].indirect(t["offsets"][:]))

        def move_rows(quad, cols):
            nc.sync.dma_start(planes[32 * quad : 32 * quad + 4, :, cols].bitcast(I32), got_scales[8 * quad : 8 * quad + 8, cols].bitcast(I32))

        def score_pass(t, o, cols, words, start, stop):
            nc.tensor.matmul_mx(
                out=t["acc"][:, cols],
                lhsT=q_codes[:, o * NQ : (o + 1) * NQ].bitcast(FP8X4),
                lhsT_scale=q_scales[:, o * NQ : (o + 1) * NQ],
                rhs=words.bitcast(FP4X4),
                rhs_scale=t["planes"][o][:, cols],
                start=start,
                stop=stop,
            )

        def cast_pass(o):
            nc.scalar.copy(
                q_bf[:, o, :].rearrange("p (m i t) -> p m t i", i=4, t=4),
                q_raw[:, o, :].rearrange("p (t m i) -> p m t i", t=4, i=4),
            )

        def part_words(pair, got):
            nc.vector.tensor_copy(pair[:].bitcast(U16), got.bitcast(U16).rearrange("p (n o) -> p o n", o=2))

        def softmax_terms(t, nmax):
            nc.vector.tensor_reduce(nmax[:], t["acc"][:], AX.X, ALU.max, negate=True)
            nc.scalar.activation(t["e"][:], t["acc"][:], ACT.Exp, bias=nmax[:], accum_out=t["total"][:])

        planes = sb.tile([P, PASSES, 2 * N], U8, align_bytes=64)
        gather_scales(c)
        for quad in range(3):
            move_rows(quad, c["cols"])
        gather_scales(k)
        move_rows(3, slice(0, 2 * N))
        for quad in range(3):
            move_rows(quad, k["cols"])
        for o in range(PASSES):
            cast_pass(o)
        for t in (c, k):
            t["planes"] = [planes[:, o, t["cols"]] for o in range(PASSES)]

        c_got = sb.tile([P, N], U32, align_bytes=64)
        nc.vector.tensor_copy(c_got[:], c["wwin"][:].bitcast(U32).indirect(c["offsets"][:]))
        nc.vector.quantize_mx(out=q_codes[:].bitcast(FP8X4), scales=q_scales[:], in_=q_bf[:].rearrange("p o x -> p (o x)"))
        c_parted = {}
        for o in range(PASSES):
            c_parted[o] = placed.tile([P, 2 * N], U8, name="c_parted%d" % o, offset=Q_RAW + 2 * N * o, align_bytes=64)
            nc.vector.tensor_copy(
                c_parted[o][:].bitcast(U16).rearrange("p (h n) -> p h n", h=2),
                c_got[:].bitcast(U16).rearrange("p (h n o) -> p o h n", h=2, o=2)[:, o],
            )
        score_pass(c, 0, slice(0, N), c_parted[0][:], True, False)
        for lo, hi in ((0, 256), (256, 384), (384, N)):
            score_pass(c, 1, slice(lo, hi), c_parted[1][:, 2 * lo : 2 * hi], False, hi == N)

        def gather_k(lo, hi):
            got = placed.tile([P, hi - lo], U32, name="k_got%d" % lo, offset=Q_BF + 4 * lo, align_bytes=64)
            nc.vector.tensor_copy(got[:], k["wwin"][:].bitcast(U32).indirect(k["offsets"][:, lo // 16 : hi // 16]))
            return got

        def score_group(lo, hi, got):
            pair = placed.tile([P, PASSES, 2 * (hi - lo)], U8, name="k_pair%d" % lo, offset=K_LAST_PAIR + 4 * (N - hi), align_bytes=64)
            part_words(pair, got)
            for o in (1, 0):
                score_pass(k, o, slice(lo, hi), pair[:, o, :], o == 1, o == 0)

        first = gather_k(0, K_FIRST)
        last = gather_k(K_FIRST, N)
        score_group(0, 128, first[:, 0:128])
        score_group(128, K_FIRST, first[:, 128:K_FIRST])
        score_group(K_FIRST, N, last[:])

        softmax_terms(c, sb.tile([P, 1], F32, name="c_nmax", align_bytes=64))
        softmax_terms(k, sb.tile([P, 1], F32, name="k_nmax", align_bytes=64))
        c_inv = placed.tile([P, 1], F32, offset=K_LAST_PAIR, align_bytes=64)
        nc.vector.reciprocal(c_inv[:], c["total"][:])
        nc.vector.tensor_scalar(part[:], c["e"][:], c_inv[:], None, ALU.mult)
        k_inv = sb.tile([P, 1], F32, align_bytes=64)
        nc.vector.reciprocal(k_inv[:], k["total"][:])
        for h in range(2):
            cols = slice(h * N // 2, (h + 1) * N // 2)
            res = sb.tile([P, N // 2], F32, name="res%d" % h, align_bytes=64)
            nc.vector.scalar_tensor_tensor(res[:], k["e"][:, cols], k_inv[:], part[:, cols], ALU.mult, ALU.add)
            nc.sync.dma_start(out[0][:, cols], res[:])
